import numpy as np, ml_dtypes
CORES = [211,219,227,235,243,251,83,91,99,107,115,123]
N = 12
import mx_ref
BF = ml_dtypes.bfloat16
def entries(a):
    return np.ascontiguousarray(a.T).reshape(-1)
def table(e):
    return np.ascontiguousarray(np.reshape(e, (-1, 16)).T).astype(np.int32)
def f(rng, *shape):
    return mx_ref.flush((rng.standard_normal(shape, dtype=np.float32) * np.exp2(rng.integers(-2, 3, shape[:-1] + (1,)))).astype(BF))
def wide(rng, *shape, cols=0):
    v = rng.standard_normal(shape, dtype=np.float32) * np.exp2(rng.integers(-12, 13, shape)).astype(np.float32)
    if cols: v *= np.repeat(np.exp2(rng.integers(-cols, cols + 1, shape[:-2] + (1, shape[-1] // 4))) * (rng.random(shape[:-2] + (1, shape[-1] // 4)) > 0.0625), 4, axis=-1).astype(np.float32)
    return mx_ref.flush(v.astype(BF))
T, CAPP, OC, UN = 192, 16, 84, 48
HOST = [0 if c < 128 else 1 for c in CORES]
def term(a, B):
    return np.stack([mx_ref.matmul(mx_ref.quantize(a[:, 512 * i:512 * i + 512]), B) for i in range(4)], axis=2).reshape(128, -1)
def padded(e, k):
    return table(np.concatenate([e, np.full(k - len(e), -1)]))
def lists(rng, fixed=False, blocks=False, plain=False, short=False):
    own = [[[] for d in range(N)] for r in range(N)]
    union = np.full((N, 2, UN), -1)
    for d in range(N):
        half = np.arange(OC) if blocks else rng.permutation(OC)
        ext = [rng.choice(half[(1 - g) * (OC // 2):(2 - g) * (OC // 2)], UN - OC // 2, replace=False) for g in range(2)]
        low = int(rng.integers(0, 2)) if short else -1
        for g in range(2):
            R = [r for r in range(N) if HOST[r] == g]
            mine = list(half[g * (OC // 2):(g + 1) * (OC // 2)]) + list(ext[g])
            p = rng.permutation(len(R)); named = [set() for _ in mine]
            for k in range(CAPP):
                if not fixed: p = rng.permutation(len(R))
                for i in range(len(R) // 2): named[k * (len(R) // 2) + i] = {R[p[2 * i]], R[p[2 * i + 1]]}
            if g == low:
                both = [j for j in range(UN) if j >= OC // 2 or mine[j] in ext[1 - g]]
                for j in both:
                    for r in list(named[j]):
                        to = [t for t in range(OC // 2) if t not in both and r not in named[t]]
                        named[j].remove(r); named[rng.choice(to)].add(r)
            elif not (plain or fixed or short):
                for j in range(OC // 2, UN):
                    for r in list(rng.permutation(list(named[j])))[:rng.integers(0, 3)]:
                        to = [t for t in range(OC // 2) if r not in named[t]]
                        named[j].remove(r); named[rng.choice(to)].add(r)
            at = rng.permutation(UN)
            for j, s in enumerate(named):
                if s: union[d, g, at[j]] = mine[j]
                for r in s: own[r][d].append((mine[j], at[j]))
    send, place, un = [], np.full((N, N, CAPP), -1), []
    for r in range(N):
        send.append(table(rng.permutation(T))); u = []
        for d in range(N):
            o = [own[r][d][i] for i in rng.permutation(CAPP)]
            place[d, r] = [v for v, _ in o]; u += [w for _, w in o]
        un.append(table(u))
    return {"send": np.stack(send), "place": np.stack([table(place[d].reshape(-1)) for d in range(N)]), "un": np.stack(un), "upl": np.stack([padded(union[d].reshape(-1), 96) for d in range(N)])}
def setup_inputs(rng):
    return {"a": f(rng, N, 128, 4 * 512), "b": f(rng, N, 128, 4 * T), **lists(rng)}
def setup_inputs_blocks(rng):
    return {**setup_inputs(rng), **lists(rng, blocks=True, plain=True)}
def setup_inputs_lossless(rng):
    d = setup_inputs(rng)
    a = np.zeros((N, 128, 4 * 128, 4), np.float32)
    for r in range(N):
        k = rng.integers(0, 512, size=4 * 128)
        a[r, k // 4, np.arange(4 * 128), k % 4] = 1.0
    size = 2.0 ** rng.integers(-4, 5, size=(N, OC)); b = rng.integers(-1, 2, size=(N, 128, T, 4)).astype(np.float64)
    for r in range(N):
        s = entries(d["send"][r]).reshape(N, CAPP)
        for o in range(N): b[r][:, s[o]] *= size[o][entries(d["place"][o]).reshape(N, CAPP)[r]][None, :, None]
    d["a"], d["b"] = a.reshape(N, 128, 4 * 512).astype(BF), b.reshape(N, 128, 4 * T).astype(np.float32).astype(BF)
    return d
def setup_inputs_pairs(rng):
    return {**setup_inputs(rng), **lists(rng, fixed=True)}
def setup_inputs_short(rng):
    return {**setup_inputs(rng), **lists(rng, short=True)}
def setup_inputs_spread(rng):
    d = setup_inputs(rng); d["b"] = wide(rng, N, 128, 4 * T); return d
def check_inputs(x):
    b = []
    seen = np.zeros((N, OC), int)
    for r in range(N):
        s, u = entries(x["send"][r]), entries(x["un"][r]).reshape(N, CAPP)
        if sorted(s.tolist()) != list(range(T)): b.append("send")
        if u.min() < 0 or u.max() >= UN: b.append("un")
        for o in range(N):
            p = entries(x["place"][o]).reshape(N, CAPP)[r]
            if p.min() < 0 or p.max() >= OC or len(set(p.tolist())) != CAPP: b.append("place")
            w = entries(x["upl"][o])[:2 * UN].reshape(2, UN)[HOST[r]]
            if (w[u[o]] != p).any(): b.append("upl")
            seen[o][p] += 1
    for o in range(N):
        for g in range(2):
            w = entries(x["upl"][o]); bad = w.min() < -1 or w.max() >= OC or (w[2 * UN:] != -1).any(); w = w[:2 * UN].reshape(2, UN)[g]; w = w[w >= 0]
            if len(set(w.tolist())) != len(w): b.append("upl twice")
    if seen.min() < 2: b.append("a column with fewer than two terms")
    return b
def reference(a, b, send, place, un, upl):
    Z = [term(a[r], mx_ref.quantize(b[r])).reshape(128, T, 4) for r in range(N)]
    y = np.zeros((N, 128, 4 * OC), np.float32)
    for o in range(N):
        parts = []
        for r in range(N):
            t = np.zeros((128, OC, 4), np.float32); t[:, entries(place[o]).reshape(N, CAPP)[r]] = Z[r][:, entries(send[r]).reshape(N, CAPP)[o]]
            parts.append(t.reshape(128, 4 * OC))
        y[o] = mx_ref.total(parts)
    return {"y": y}

@@ -1,0 +1,300 @@
+import numpy as np
+from concourse.bass import DstId, RemoteDMATransfer
+from concourse.mybir import dt, AluOpType, ActivationFunctionType
+
+UN, OC, H = 48, 84, 6
+SITE = 2 * UN
+SLOT = SITE + 128
+WIN = 304
+SEC = 52
+
+F32, BF, I32, U16, X4, U8 = "float32", "bfloat16", "int32", "uint16", "float8_e4m3fn_x4", "uint8"
+SCRATCH = {
+    "lsend": ("sbuf", [128, 12], I32), "lun": ("sbuf", [128, 12], I32), "lupl": ("sbuf", [128, 6], I32),
+    "base": ("sbuf", [128, 12], I32), "uo": ("sbuf", [128, 12], I32),
+    "gofs": ("sbuf", [128, 12], U16), "sofs": ("sbuf", [128, 48], U16),
+    "bt": ("sbuf", [128, 768], BF), "at": ("sbuf", [128, 2048], BF),
+    "bc1": ("sbuf", [128, 256], BF), "bp": ("sbuf", [128, 768], BF), "bc2": ("sbuf", [128, 512], BF),
+    "qa": ("sbuf", [128, 512], X4), "sa": ("sbuf", [128, 512], U8),
+    "qb1": ("sbuf", [128, 192], X4), "sb1": ("sbuf", [128, 192], U8),
+    "qb2": ("sbuf", [128, 128], X4), "sb2": ("sbuf", [128, 128], U8),
+    "ones": ("sbuf", [128, 520], BF), "strip": ("sbuf", [128, 520], BF), "zt": ("sbuf", [128, 512], BF),
+    "qe": ("sbuf", [128, 512], X4), "se": ("sbuf", [128, 512], U8),
+    "zc": ("sbuf", [128, 512], BF),
+    "h1": ("sbuf", [128, 768], BF), "h2": ("sbuf", [128, 768], BF), "h3": ("sbuf", [128, 896], BF),
+    "qh1": ("sbuf", [128, 192], X4), "sh1": ("sbuf", [128, 192], U8),
+    "qh2": ("sbuf", [128, 192], X4), "sh2": ("sbuf", [128, 192], U8),
+    "qh3": ("sbuf", [128, 224], X4), "sh3": ("sbuf", [128, 224], U8),
+    "land": ("sbuf", [128, 5 * SLOT], X4), "lsc": ("sbuf", [128, 5 * SLOT], U8),
+    "mt": ("sbuf", [128, 512], BF), "qm": ("sbuf", [128, 128], X4), "sm": ("sbuf", [128, 128], U8),
+    "rl": ("sbuf", [128, UN + 128], X4), "rs": ("sbuf", [128, UN + 128], U8),
+    "lf": ("sbuf", [128, 4 * SEC], F32), "rf": ("sbuf", [128, 4 * SEC], F32),
+    "yacc": ("sbuf", [128, 384], F32), "yo": ("sbuf", [128, 384], F32),
+    "jc": ("sbuf", [128, 6], I32), "neg": ("sbuf", [128, 6], I32), "dump": ("sbuf", [128, 6], I32),
+    "uplo": ("sbuf", [128, 6], I32), "uofs": ("sbuf", [128, 8], U16), "wv": ("sbuf", [128, UN], F32),
+    "win": ("sbuf", [128, 2 * WIN], F32), "mi": ("sbuf", [128, 96], I32), "mj": ("sbuf", [128, 96], I32),
+    "mask": ("sbuf", [128, 96], F32), "d0": ("sbuf", [128, 192], F32), "dm": ("sbuf", [128, 192], F32),
+    "ds": ("sbuf", [128, 192], F32), "iofs": ("sbuf", [128, 12], U16),
+    "px": ("psum", [128, 2048], F32), "py": ("psum", [128, 2048], F32),
+}
+SEMAPHORES = ["gs", "vs", "ss", "ts", "ldsend", "ldun", "ldupl", "ldb", "lda0", "lda1", "stored", "sent", "xarr"] + ["arr%d" % x for x in range(H)]
+
+
+def rank_program(g, core, T, topo):
+    rank = T.rank_of(core)
+    if rank is None:
+        return
+    V, S, P, Y = g.vector, g.scalar, g.tensor, g.sync
+    COPY = ActivationFunctionType.Copy
+    half, me = rank // H, rank % H
+    pair, odd = me // 2, me % 2
+    peers = [T.cores[half * H + x] for x in range(H)]
+    host = topo.host(core)
+
+    count = {"gs": 0, "vs": 0, "ss": 0, "ts": 0}
+    queues = {"g": g, "v": V, "s": S, "t": P, "y": Y}
+    known = {q: {} for q in queues}
+
+    def done(sem, ins):
+        ins.then_inc(T.sem[sem], 1)
+        count[sem] += 1
+        return (sem, count[sem])
+
+    def need(q, *tokens):
+        best = {}
+        for sem, n in tokens:
+            best[sem] = max(n, best.get(sem, 0))
+        for sem, n in best.items():
+            if known[q].get(sem, 0) < n:
+                queues[q].wait_ge(T.sem[sem], n)
+                known[q][sem] = n
+
+    S.dma_start(T.bt[:], T.b[:]).then_inc(T.sem.ldb, 16)
+    for k in range(8):
+        Y.dma_start(T.lsend[16 * k:16 * k + 16, :], T.send[:]).then_inc(T.sem.ldsend, 16)
+    for k in range(8):
+        S.dma_start(T.lun[16 * k:16 * k + 16, :], T.un[:]).then_inc(T.sem.ldun, 16)
+    Y.dma_start(T.at[:, 0:1024], T.a[:, 0:1024]).then_inc(T.sem.lda0, 16)
+    S.dma_start(T.at[:, 1024:2048], T.a[:, 1024:2048]).then_inc(T.sem.lda1, 16)
+    for k in range(8):
+        Y.dma_start(T.lupl[16 * k:16 * k + 16, :], T.upl[:]).then_inc(T.sem.ldupl, 16)
+    LSEND, LUN, LUPL, LB, LA0, LA1 = ("ldsend", 128), ("ldun", 128), ("ldupl", 128), ("ldb", 16), ("lda0", 16), ("lda1", 16)
+
+    k_base = done("gs", g.iota(T.base[:], [[UN, 2], [0, 3], [SITE, 2]], 0, 0))
+    k_ones = done("vs", V.memset(T.ones[:], 1.0))
+    need("g", k_ones)
+    k_strip = done("gs", g.affine_select(T.strip[:], T.ones[:], [[1, 520]], AluOpType.is_equal, 0.0, -4, -4))
+    k_jc = done("gs", g.iota(T.jc[:], [[16, 6]], 97, 1))
+    k_wv = done("gs", g.iota(T.wv[:], [[1, UN]], 0, 0, allow_small_or_imprecise_dtypes=True))
+    k_mi = done("gs", g.iota(T.mi[:], [[1, 96]], 128, -1))
+    k_bp0 = done("vs", V.memset(T.bp[:], 0.0))
+    k_h20 = done("vs", V.memset(T.h2[:], 0.0))
+    k_h30 = done("vs", V.memset(T.h3[:], 0.0))
+    need("v", k_strip)
+    for t in range(4):
+        k_e = done("vs", V.quantize_mx(T.qe[:, 128 * t:128 * t + 128], T.se[:, 128 * t:128 * t + 128], T.strip[:, 4 - t:516 - t]))
+
+    groups = [(pair + 1) % 3, (pair + 2) % 3, pair]
+
+    def picks(k):
+        for h in range(2):
+            c = H * h + 2 * groups[k]
+            tok = done("vs", V.tensor_scalar(T.gofs[:, 4 * k + 2 * h:4 * k + 2 * h + 2], T.lsend[:, c:c + 2], 4, None, AluOpType.mult))
+        return tok
+
+    def places(k):
+        for h in range(2):
+            c = H * h + 2 * groups[k]
+            tok = done("vs", V.tensor_scalar(T.sofs[:, 16 * k + 2 * h:16 * k + 2 * h + 2], T.uo[:, c:c + 2], 4, None, AluOpType.mult))
+        need("v", tok)
+        for t in (1, 2, 3):
+            tok = done("vs", V.tensor_scalar(T.sofs[:, 16 * k + 4 * t:16 * k + 4 * t + 4], T.sofs[:, 16 * k:16 * k + 4], t, None, AluOpType.add))
+        return tok
+
+    need("v", LSEND)
+    k_g1 = picks(0)
+    need("v", LUN, k_base)
+    k_uo = done("vs", V.tensor_tensor(T.uo[:], T.lun[:], T.base[:], AluOpType.add))
+    picks(1)
+    k_g23 = picks(2)
+    need("v", k_uo)
+    k_s1 = places(0)
+
+    need("s", LB, k_g1)
+    k_bc1 = [done("ss", S.activation(T.bc1[:, 64 * t:64 * t + 64], T.bt[:, t:768].indirect(T.gofs[:, 0:4]), COPY)) for t in range(4)]
+    need("s", k_g23)
+    for t in range(4):
+        k_bc2 = done("ss", S.activation(T.bc2[:, t:512:4], T.bt[:, t:768].indirect(T.gofs[:, 4:12]), COPY))
+    k_bp = k_bp0
+    for u in range(2):
+        need("v", k_bp, k_s1, k_bc1[2 * u + 1])
+        k_bp = done("vs", V.tensor_copy(T.bp[:].indirect(T.sofs[:, 8 * u:8 * u + 8]), T.bc1[:, 128 * u:128 * u + 128]))
+    need("v", k_bp)
+    k_qb1 = done("vs", V.quantize_mx(T.qb1[:], T.sb1[:], T.bp[:]))
+    k_qa = []
+    for u, load in enumerate((LA0, LA1)):
+        need("v", load)
+        k_qa.append(done("vs", V.quantize_mx(T.qa[:, 256 * u:256 * u + 256], T.sa[:, 256 * u:256 * u + 256], T.at[:, 1024 * u:1024 * u + 1024])))
+    need("v", k_bc2)
+    k_qb2 = done("vs", V.quantize_mx(T.qb2[:], T.sb2[:], T.bc2[:]))
+
+    k_px, k_py = [], []
+    need("t", k_qb1)
+    for i in range(4):
+        need("t", k_qa[i // 2])
+        k_px.append(done("ts", P.matmul_mx(T.px[:, 512 * i:512 * i + 192], T.qa[:, 128 * i:128 * i + 128], T.sa[:, 128 * i:128 * i + 128], T.qb1[:], T.sb1[:], True, True)))
+    need("t", k_qb2)
+    for i in range(4):
+        k_py.append(done("ts", P.matmul_mx(T.py[:, 512 * i:512 * i + 128], T.qa[:, 128 * i:128 * i + 128], T.sa[:, 128 * i:128 * i + 128], T.qb2[:], T.sb2[:], True, True)))
+
+    for i in (0, 2):
+        need("v", k_px[i])
+        k_c1v = done("vs", V.tensor_copy(T.h1[:, i:768:4], T.px[:, 512 * i:512 * i + 192]))
+    for i in (1, 3):
+        need("s", k_px[i])
+        k_c1s = done("ss", S.activation(T.h1[:, i:768:4], T.px[:, 512 * i:512 * i + 192], COPY))
+    need("v", k_c1v, k_c1s)
+    k_h1 = done("vs", V.quantize_mx(T.qh1[:], T.sh1[:], T.h1[:]))
+    k_zc = []
+    for k in range(2):
+        for t in range(4):
+            need("s", k_py[t])
+            tok = done("ss", S.activation(T.zc[:, 256 * k + 64 * t:256 * k + 64 * t + 64], T.py[:, 512 * t + 64 * k:512 * t + 64 * k + 64], COPY))
+        k_zc.append(tok)
+    k_s2 = places(1)
+    k_s3 = places(2)
+    need("v", k_s2, k_h20, k_zc[0])
+    k_c2 = done("vs", V.tensor_copy(T.h2[:].indirect(T.sofs[:, 16:32]), T.zc[:, 0:256]))
+    need("v", k_c2)
+    k_h2 = done("vs", V.quantize_mx(T.qh2[:], T.sh2[:], T.h2[:]))
+    need("v", k_s3, k_h30, k_zc[1])
+    k_c3 = done("vs", V.tensor_copy(T.h3[:].indirect(T.sofs[:, 32:48]), T.zc[:, 256:512]))
+    need("v", k_c3)
+    k_h3 = done("vs", V.quantize_mx(T.qh3[:], T.sh3[:], T.h3[:]))
+
+    def bits(engines):
+        return sum(1 << e for e in engines)
+
+    def slot(receiver, sender):
+        return SLOT * (sender if sender < receiver else sender - 1)
+
+    def transfer(x, engines, src, dst):
+        rid, pid = topo.addr(peers[x], core)
+        return RemoteDMATransfer(dst_ids=[DstId(rid=rid, pnc=pid)], dma_engine_mask=bits(engines), remote_sem=T.sem["arr%d" % me], srcs=[src], dsts=[dst])
+
+    sent = 0
+    for k, (tok, qh, sh) in enumerate(((k_h1, T.qh1, T.sh1), (k_h2, T.qh2, T.sh2))):
+        need("g", tok)
+        for plane in range(2):
+            ts = []
+            for e in range(2):
+                x = 2 * groups[k] + e
+                eng = topo.engines(core, peers[x])
+                q = len(eng) // 4
+                part = 2 * ((k + plane) % 2) + e
+                at = slot(x, me)
+                if plane:
+                    src, dst = sh[:, SITE * e:SITE * e + SITE], T.lsc[:, at:at + SITE]
+                else:
+                    src, dst = qh[:, SITE * e:SITE * e + SITE].bitcast(dt.uint8), T.land[:, at:at + SITE].bitcast(dt.uint8)
+                ts.append(transfer(x, eng[q * part:q * part + q], src, dst))
+                sent += q
+            g.remote_dma_fused(ts, local_sem=T.sem.sent)
+    mate = me + 1 - 2 * odd
+    eng = topo.engines(core, peers[mate])
+    rid, pid = topo.addr(peers[mate], core)
+    at, lo = slot(mate, me), SITE * (1 - odd)
+    need("g", k_h3)
+    g.remote_dma(T.land[:, at:at + SITE].bitcast(dt.uint8), T.qh3[:, lo:lo + SITE].bitcast(dt.uint8), T.sem["arr%d" % me], T.sem.sent, pid, rid, bits(eng))
+    g.remote_dma(T.lsc[:, at:at + SITE], T.sh3[:, lo:lo + SITE], T.sem["arr%d" % me], T.sem.sent, pid, rid, bits(eng))
+    sent += 2 * len(eng)
+
+    k_zt = done("vs", V.memset(T.zt[:], 0.0))
+    need("v", k_zt)
+    for k in range(5):
+        k_pad = done("vs", V.quantize_mx(T.land[:, SLOT * k + SITE:SLOT * (k + 1)], T.lsc[:, SLOT * k + SITE:SLOT * (k + 1)], T.zt[:]))
+    k_rpad = done("vs", V.quantize_mx(T.rl[:, UN:UN + 128], T.rs[:, UN:UN + 128], T.zt[:]))
+
+    def decode(t, out, codes, scales, c, start, stop):
+        return done("ts", P.matmul_mx(out[:, 512 * t:512 * t + 128], T.qe[:, 128 * t:128 * t + 128], T.se[:, 128 * t:128 * t + 128], codes[:, c:c + 128], scales[:, c:c + 128], start, stop))
+
+    need("t", k_h3, k_e, k_c1v, k_c1s)
+    for t in range(4):
+        decode(t, T.px, T.qh3, T.sh3, SITE * odd, True, False)
+    need("t", k_pad)
+    n8 = len(eng)
+    first, second = (pair + 2) % 3, (pair + 1) % 3
+    for x, n in ((2 * first, n8 // 2), (2 * first + 1, n8 // 2), (2 * second, n8 // 2), (2 * second + 1, n8 // 2), (mate, 2 * n8)):
+        P.wait_ge(T.sem["arr%d" % x], n)
+        k_acc = [decode(t, T.px, T.land, T.lsc, slot(me, x), False, x == mate) for t in range(4)]
+
+    k_mt = done("vs", V.memset(T.mt[:, 4 * UN:512], 0.0))
+    for t in range(4):
+        done("vs", V.memset(T.lf[:, SEC * t + UN:SEC * t + SEC], 0.0))
+        k_z0 = done("vs", V.memset(T.rf[:, SEC * t + UN:SEC * t + SEC], 0.0))
+    k_win = done("vs", V.memset(T.win[:], float(UN)))
+    k_d1 = done("vs", V.memset(T.d0[:], 1.0))
+    need("v", LUPL, k_jc, k_wv, k_mi)
+    k_ng = done("vs", V.tensor_scalar(T.neg[:], T.lupl[:], 0, None, AluOpType.is_lt))
+    k_mj = done("vs", V.tensor_scalar(T.mj[:], T.mi[:], 15, None, AluOpType.bitwise_and))
+    need("v", k_ng)
+    k_dp = done("vs", V.tensor_tensor(T.dump[:], T.neg[:], T.jc[:], AluOpType.mult))
+    k_d0 = done("vs", V.memset(T.d0[:, 0:192:16], 0.0))
+    need("v", k_dp)
+    k_uo2 = done("vs", V.tensor_tensor(T.uplo[:], T.lupl[:], T.dump[:], AluOpType.add))
+    k_mk = done("vs", V.tensor_scalar(T.mask[:], T.mj[:], 0, None, AluOpType.is_equal))
+    need("v", k_uo2)
+    for q in range(2):
+        k_uf = done("vs", V.tensor_copy(T.uofs[:, 4 * q:4 * q + 3], T.uplo[:, 3 * q:3 * q + 3]))
+    need("v", k_uf, k_win)
+    for q in range(2):
+        k_sc = done("vs", V.tensor_copy(T.win[:, WIN * q:WIN * q + WIN].indirect(T.uofs[:, 4 * q:4 * q + 3]), T.wv[:]))
+    need("v", k_sc, k_mk)
+    for q in range(2):
+        k_dm = done("vs", V.tensor_tensor(T.dm[:, 96 * q:96 * q + 96], T.win[:, WIN * q:WIN * q + 96], T.mask[:], AluOpType.mult))
+    need("v", k_dm, k_d0)
+    k_ds = done("vs", V.tensor_tensor_scan(T.ds[:], T.d0[:], T.dm[:], 0.0, AluOpType.mult, AluOpType.add))
+    need("v", k_ds)
+    k_io = done("vs", V.tensor_copy(T.iofs[:], T.ds[:, 15:192:16]))
+
+    far = UN * (1 - half)
+    for t in (0, 2):
+        need("v", k_acc[t])
+        k_mv = done("vs", V.tensor_copy(T.mt[:, t:4 * UN:4], T.px[:, 512 * t + far:512 * t + far + UN]))
+    for t in (1, 3):
+        need("s", k_acc[t])
+        k_ms = done("ss", S.activation(T.mt[:, t:4 * UN:4], T.px[:, 512 * t + far:512 * t + far + UN], COPY))
+    need("v", k_mv, k_ms, k_mt)
+    k_qm = done("vs", V.quantize_mx(T.qm[:], T.sm[:], T.mt[:]))
+    other = T.cores[(rank + H) % (2 * H)]
+    rid, pid = topo.addr(other, core)
+    eng = topo.engines(core, other)
+    need("g", k_qm)
+    g.remote_dma(T.rl[:, 0:UN].bitcast(dt.uint8), T.qm[:, 0:UN].bitcast(dt.uint8), T.sem.xarr, T.sem.sent, pid, rid, bits(eng))
+    g.remote_dma(T.rs[:, 0:UN], T.sm[:, 0:UN], T.sem.xarr, T.sem.sent, pid, rid, bits(eng))
+    sent += 2 * len(eng)
+
+    near = UN * half
+    need("s", k_mv, k_z0)
+    for t in range(4):
+        k_lf = done("ss", S.activation(T.lf[:, SEC * t:SEC * t + UN], T.px[:, 512 * t + near:512 * t + near + UN], COPY))
+    need("s", k_lf, k_io)
+    for t in range(4):
+        k_ya = done("ss", S.activation(T.yacc[:, t:384:4], T.lf[:, SEC * t:SEC * t + UN + 1].indirect(T.iofs[:, 6 * host:6 * host + 6]), COPY))
+
+    need("t", k_zc[1], k_rpad)
+    P.wait_ge(T.sem.xarr, 2 * len(eng))
+    k_r = [decode(t, T.py, T.rl, T.rs, 0, True, True) for t in range(4)]
+    k_rf = []
+    for t in range(4):
+        need("s", k_r[t])
+        k_rf.append(done("ss", S.activation(T.rf[:, SEC * t:SEC * t + UN], T.py[:, 512 * t:512 * t + UN], COPY)))
+    need("v", k_ya)
+    q = 6 * (1 - host)
+    for t in range(4):
+        need("v", k_rf[t])
+        k_yo = done("vs", V.tensor_tensor(T.yo[:, t:384:4], T.rf[:, SEC * t:SEC * t + UN + 1].indirect(T.iofs[:, q:q + 6]), T.yacc[:, t:384:4], AluOpType.add))
+    need("y", k_yo)
+    Y.dma_start(T.y[:], T.yo[:, 0:4 * OC]).then_inc(T.sem.stored, 16)
+
+    need("g", ("sent", sent), ("vs", count["vs"]), ("ss", count["ss"]), ("ts", count["ts"]), ("gs", count["gs"]), ("stored", 16))

@@ -4,52 +4,90 @@ from concourse.mybir import dt, AluOpType, ActivationFunctionType
 
 UN, OC, H = 48, 84, 6
 SITE = 2 * UN
-SLOT = SITE + 128
-WIN = 304
-SEC = 52
+W = 4 * SITE
+MINC = 128
+EAT = UN + 5 * SITE
+ABIG = 1536
+CUT = 10
 
 F32, BF, I32, U16, X4, U8 = "float32", "bfloat16", "int32", "uint16", "float8_e4m3fn_x4", "uint8"
 SCRATCH = {
-    "lsend": ("sbuf", [128, 12], I32), "lun": ("sbuf", [128, 12], I32), "lupl": ("sbuf", [128, 6], I32),
-    "base": ("sbuf", [128, 12], I32), "uo": ("sbuf", [128, 12], I32),
-    "gofs": ("sbuf", [128, 12], U16), "sofs": ("sbuf", [128, 48], U16),
+    "lists": ("sbuf", [128, 24], I32), "lupl": ("sbuf", [128, 6], I32),
+    "pc": ("sbuf", [128, 1], I32), "bits": ("sbuf", [128, 4], I32), "bitf": ("sbuf", [128, 4], F32),
+    "colb": ("sbuf", [128, 4], I32), "cof": ("sbuf", [128, 4], U16),
+    "kk": ("sbuf", [128, 64], F32), "k4": ("sbuf", [128, 64], F32),
+    "off": ("sbuf", [128, 64], F32), "ofs": ("sbuf", [128, 64], U16), "g2": ("sbuf", [128, 10], U16),
     "bt": ("sbuf", [128, 768], BF), "at": ("sbuf", [128, 2048], BF),
-    "bc1": ("sbuf", [128, 256], BF), "bp": ("sbuf", [128, 768], BF), "bc2": ("sbuf", [128, 512], BF),
+    "bc1": ("sbuf", [128, 128], BF), "bp": ("sbuf", [128, 512], BF), "bc2": ("sbuf", [128, 640], BF),
     "qa": ("sbuf", [128, 512], X4), "sa": ("sbuf", [128, 512], U8),
-    "qb1": ("sbuf", [128, 192], X4), "sb1": ("sbuf", [128, 192], U8),
-    "qb2": ("sbuf", [128, 128], X4), "sb2": ("sbuf", [128, 128], U8),
-    "ones": ("sbuf", [128, 520], BF), "strip": ("sbuf", [128, 520], BF), "zt": ("sbuf", [128, 512], BF),
+    "qb1": ("sbuf", [128, 128], X4), "sb1": ("sbuf", [128, 128], U8),
+    "qb2": ("sbuf", [128, 160], X4), "sb2": ("sbuf", [128, 160], U8),
+    "ones": ("sbuf", [128, 520], BF), "strip": ("sbuf", [128, 520], BF),
     "qe": ("sbuf", [128, 512], X4), "se": ("sbuf", [128, 512], U8),
-    "zc": ("sbuf", [128, 512], BF),
-    "h1": ("sbuf", [128, 768], BF), "h2": ("sbuf", [128, 768], BF), "h3": ("sbuf", [128, 896], BF),
-    "qh1": ("sbuf", [128, 192], X4), "sh1": ("sbuf", [128, 192], U8),
-    "qh2": ("sbuf", [128, 192], X4), "sh2": ("sbuf", [128, 192], U8),
-    "qh3": ("sbuf", [128, 224], X4), "sh3": ("sbuf", [128, 224], U8),
-    "land": ("sbuf", [128, 5 * SLOT], X4), "lsc": ("sbuf", [128, 5 * SLOT], U8),
+    "zc": ("sbuf", [128, 640], BF), "h": ("sbuf", [128, 6 * W + 128], BF),
+    "qh": ("sbuf", [128, 6 * MINC], X4), "sh": ("sbuf", [128, 6 * MINC], U8),
+    "land": ("sbuf", [128, EAT + 512], X4), "lsc": ("sbuf", [128, EAT + 512], U8),
     "mt": ("sbuf", [128, 512], BF), "qm": ("sbuf", [128, 128], X4), "sm": ("sbuf", [128, 128], U8),
-    "rl": ("sbuf", [128, UN + 128], X4), "rs": ("sbuf", [128, UN + 128], U8),
-    "lf": ("sbuf", [128, 4 * SEC], F32), "rf": ("sbuf", [128, 4 * SEC], F32),
-    "yacc": ("sbuf", [128, 384], F32), "yo": ("sbuf", [128, 384], F32),
-    "jc": ("sbuf", [128, 6], I32), "neg": ("sbuf", [128, 6], I32), "dump": ("sbuf", [128, 6], I32),
-    "uplo": ("sbuf", [128, 6], I32), "uofs": ("sbuf", [128, 8], U16), "wv": ("sbuf", [128, UN], F32),
-    "win": ("sbuf", [128, 2 * WIN], F32), "mi": ("sbuf", [128, 96], I32), "mj": ("sbuf", [128, 96], I32),
-    "mask": ("sbuf", [128, 96], F32), "d0": ("sbuf", [128, 192], F32), "dm": ("sbuf", [128, 192], F32),
-    "ds": ("sbuf", [128, 192], F32), "iofs": ("sbuf", [128, 12], U16),
+    "lf": ("sbuf", [128, 4 * UN + 4], F32), "rf": ("sbuf", [128, 4 * UN + 4], F32),
+    "yacc": ("sbuf", [128, 4 * OC], F32), "yo": ("sbuf", [128, 4 * OC], F32),
+    "dump": ("sbuf", [128, 6], I32), "neg": ("sbuf", [128, 6], I32), "uplo": ("sbuf", [128, 6], I32),
+    "uofs": ("sbuf", [128, 6], U16), "wv": ("sbuf", [128, SITE], F32), "win": ("sbuf", [128, 376], F32),
+    "d0": ("sbuf", [128, 2 * OC], F32), "mask": ("sbuf", [128, 2 * OC], F32), "dm": ("sbuf", [128, 2 * OC], F32),
+    "ds": ("sbuf", [128, 2 * OC], F32), "iofs": ("sbuf", [128, 44], U16),
     "px": ("psum", [128, 2048], F32), "py": ("psum", [128, 2048], F32),
 }
-SEMAPHORES = ["gs", "vs", "ss", "ts", "ldsend", "ldun", "ldupl", "ldb", "lda0", "lda1", "stored", "sent", "xarr"] + ["arr%d" % x for x in range(H)]
+SEMAPHORES = ["gs", "vs", "ss", "ts", "ldl", "ldupl", "ldb", "lda0", "lda1", "stored", "sent", "xarr", "earr"] + ["arr%d" % k for k in range(5)]
+
+
+def helper_of(c, T, topo):
+    return min(o for o in topo.cores_of(c) if o not in T.cores and topo.die(o) == topo.die(c))
+
+
+def stages(x, peers, topo):
+    ring = [(x + s) % H for s in range(1, H)]
+    mate = [o for o in ring if topo.mates(peers[x], peers[o])]
+    plane = [o for o in ring if topo.same_plane(peers[x], peers[o])]
+    return [o for o in ring if o not in mate + plane] + plane + mate
+
+
+def bits_of(engines):
+    return sum(1 << e for e in engines)
+
+
+def helper_program(g, core, target, T, topo):
+    V = g.vector
+    V.memset(T.ones[:], 1.0).then_inc(T.sem.vs, 1)
+    g.wait_ge(T.sem.vs, 1)
+    g.affine_select(T.strip[:], T.ones[:], [[1, 520]], AluOpType.is_equal, 0.0, -4, -4).then_inc(T.sem.gs, 1)
+    V.wait_ge(T.sem.gs, 1)
+    for t in range(4):
+        V.quantize_mx(T.qe[:, 128 * t:128 * t + 128], T.se[:, 128 * t:128 * t + 128], T.strip[:, 4 - t:516 - t]).then_inc(T.sem.vs, 1)
+    g.wait_ge(T.sem.vs, 5)
+    rid, pid = topo.addr(target, core)
+    eng = topo.engines(core, target)
+    g.remote_dma(T.land[:, EAT:EAT + 512].bitcast(dt.uint8), T.qe[:].bitcast(dt.uint8), T.sem.earr, T.sem.sent, pid, rid, bits_of(eng))
+    g.remote_dma(T.lsc[:, EAT:EAT + 512], T.se[:], T.sem.earr, T.sem.sent, pid, rid, bits_of(eng))
+    g.wait_ge(T.sem.sent, 2 * len(eng))
+    g.wait_ge(T.sem.gs, 1)
 
 
 def rank_program(g, core, T, topo):
     rank = T.rank_of(core)
     if rank is None:
+        for c in T.cores:
+            if helper_of(c, T, topo) == core:
+                helper_program(g, core, c, T, topo)
         return
     V, S, P, Y = g.vector, g.scalar, g.tensor, g.sync
     COPY = ActivationFunctionType.Copy
+    ADD, MULT, AND, SHR = AluOpType.add, AluOpType.mult, AluOpType.bitwise_and, AluOpType.logical_shift_right
+    FLT = {"allow_small_or_imprecise_dtypes": True}
     half, me = rank // H, rank % H
-    pair, odd = me // 2, me % 2
     peers = [T.cores[half * H + x] for x in range(H)]
     host = topo.host(core)
+    order = stages(me, peers, topo) + [me]
+    first = order[0]
+    compact = [x for x in range(H) if x != first]
 
     count = {"gs": 0, "vs": 0, "ss": 0, "ts": 0}
     queues = {"g": g, "v": V, "s": S, "t": P, "y": Y}
@@ -69,195 +107,168 @@ def rank_program(g, core, T, topo):
                 queues[q].wait_ge(T.sem[sem], n)
                 known[q][sem] = n
 
-    S.dma_start(T.bt[:], T.b[:]).then_inc(T.sem.ldb, 16)
-    for k in range(8):
-        Y.dma_start(T.lsend[16 * k:16 * k + 16, :], T.send[:]).then_inc(T.sem.ldsend, 16)
-    for k in range(8):
-        S.dma_start(T.lun[16 * k:16 * k + 16, :], T.un[:]).then_inc(T.sem.ldun, 16)
-    Y.dma_start(T.at[:, 0:1024], T.a[:, 0:1024]).then_inc(T.sem.lda0, 16)
-    S.dma_start(T.at[:, 1024:2048], T.a[:, 1024:2048]).then_inc(T.sem.lda1, 16)
+    for k in range(2):
+        Y.dma_start(T.lists[16 * k:16 * k + 16, 0:12], T.send[:]).then_inc(T.sem.ldl, 16)
+        S.dma_start(T.lists[16 * k:16 * k + 16, 12:24], T.un[:]).then_inc(T.sem.ldl, 16)
+    Y.dma_start(T.bt[:], T.b[:]).then_inc(T.sem.ldb, 16)
+    Y.dma_start(T.at[:, 0:ABIG], T.a[:, 0:ABIG]).then_inc(T.sem.lda0, 16)
+    Y.dma_start(T.at[:, ABIG:2048], T.a[:, ABIG:2048]).then_inc(T.sem.lda1, 16)
     for k in range(8):
         Y.dma_start(T.lupl[16 * k:16 * k + 16, :], T.upl[:]).then_inc(T.sem.ldupl, 16)
-    LSEND, LUN, LUPL, LB, LA0, LA1 = ("ldsend", 128), ("ldun", 128), ("ldupl", 128), ("ldb", 16), ("lda0", 16), ("lda1", 16)
+    LL, LUPL, LB, LA0, LA1 = ("ldl", 64), ("ldupl", 128), ("ldb", 16), ("lda0", 16), ("lda1", 16)
 
-    k_base = done("gs", g.iota(T.base[:], [[UN, 2], [0, 3], [SITE, 2]], 0, 0))
-    k_ones = done("vs", V.memset(T.ones[:], 1.0))
-    need("g", k_ones)
-    k_strip = done("gs", g.affine_select(T.strip[:], T.ones[:], [[1, 520]], AluOpType.is_equal, 0.0, -4, -4))
-    k_jc = done("gs", g.iota(T.jc[:], [[16, 6]], 97, 1))
-    k_wv = done("gs", g.iota(T.wv[:], [[1, UN]], 0, 0, allow_small_or_imprecise_dtypes=True))
-    k_mi = done("gs", g.iota(T.mi[:], [[1, 96]], 128, -1))
+    k_pc = done("gs", g.iota(T.pc[:], [[0, 1]], 0, 1))
+    done("gs", g.iota(T.colb[:, 0:1], [[0, 1]], 2 * (first // 2), 0))
+    k_colb = done("gs", g.iota(T.colb[:, 1:4], [[2, 3]], 12, 0))
+    done("gs", g.iota(T.kk[:, 0:16], [[0, 2], [1, 4], [0, 2]], 0, 0, **FLT))
+    k_kk = done("gs", g.iota(T.kk[:, 16:64], [[0, 6], [1, 4], [4 * UN, 2]], 0, 0, **FLT))
+
+    def region(k):
+        return W * (5 - k)
+
+    k_z1 = done("gs", g.iota(T.h[:, region(1):region(0)], [[0, W]], 0, 0, **FLT))
+    k_z3 = done("gs", g.iota(T.h[:, region(3):region(1)], [[0, 2 * W]], 0, 0, **FLT))
+
     k_bp0 = done("vs", V.memset(T.bp[:], 0.0))
-    k_h20 = done("vs", V.memset(T.h2[:], 0.0))
-    k_h30 = done("vs", V.memset(T.h3[:], 0.0))
-    need("v", k_strip)
+    need("v", k_pc)
+    done("vs", V.tensor_scalar(T.bits[:, 0:1], T.pc[:], 1, None, AND))
+    k_b = done("vs", V.tensor_scalar(T.bits[:, 1:2], T.pc[:], 3, 1, SHR, AND))
+    k_pad = done("vs", V.memset(T.h[:, 6 * W:6 * W + 128], 0.0))
+    need("v", k_b)
+    done("vs", V.tensor_scalar(T.bitf[:, 0:1], T.bits[:, 0:1], H, None, MULT))
+    k_b = done("vs", V.tensor_copy(T.bitf[:, 1:2], T.bits[:, 1:2]))
+    need("v", k_b, k_colb)
+    k_cof = done("vs", V.tensor_scalar(T.cof[:], T.colb[:], T.bitf[:, 0:1], T.bitf[:, 1:2], ADD, ADD))
+    need("v", k_kk)
+    k_k4 = done("vs", V.tensor_scalar(T.k4[:], T.kk[:], 0.25, None, MULT))
+    need("s", k_bp0)
+    for k in (4, 5):
+        k_z5 = done("ss", S.activation(T.h[:, region(k):region(k) + W], T.bp[:, 0:W], COPY))
+
+    need("v", LL)
+    for p0 in (32, 64, 96):
+        k_l = done("vs", V.tensor_copy(T.lists[p0:p0 + 32, :], T.lists[0:32, :]))
+    need("v", k_l, k_cof, k_k4)
+    k_off = done("vs", V.tensor_tensor(T.off[:], T.lists[:].indirect(T.cof[:]), T.k4[:], ADD))
+    need("v", k_off)
+    k_ofs = done("vs", V.tensor_scalar(T.ofs[:], T.off[:], 4, None, MULT))
+    for h in range(2):
+        if first > 0:
+            k_g2 = done("vs", V.tensor_scalar(T.g2[:, h:2 * first:2], T.lists[:, H * h:H * h + first], 4, None, MULT))
+        if first < H - 1:
+            k_g2 = done("vs", V.tensor_scalar(T.g2[:, 2 * first + h:10:2], T.lists[:, H * h + first + 1:H * h + H], 4, None, MULT))
+
+    def places(x):
+        return T.ofs[:, 16 + 8 * x:24 + 8 * x]
+
+    need("s", LB, k_ofs)
+    k_bc1 = done("ss", S.activation(T.bc1[:], T.bt[:].indirect(T.ofs[:, 8 * (first % 2):8 * (first % 2) + 8]), COPY))
+    need("s", k_g2)
     for t in range(4):
-        k_e = done("vs", V.quantize_mx(T.qe[:, 128 * t:128 * t + 128], T.se[:, 128 * t:128 * t + 128], T.strip[:, 4 - t:516 - t]))
-
-    groups = [(pair + 1) % 3, (pair + 2) % 3, pair]
-
-    def picks(k):
-        for h in range(2):
-            c = H * h + 2 * groups[k]
-            tok = done("vs", V.tensor_scalar(T.gofs[:, 4 * k + 2 * h:4 * k + 2 * h + 2], T.lsend[:, c:c + 2], 4, None, AluOpType.mult))
-        return tok
-
-    def places(k):
-        for h in range(2):
-            c = H * h + 2 * groups[k]
-            tok = done("vs", V.tensor_scalar(T.sofs[:, 16 * k + 2 * h:16 * k + 2 * h + 2], T.uo[:, c:c + 2], 4, None, AluOpType.mult))
-        need("v", tok)
-        for t in (1, 2, 3):
-            tok = done("vs", V.tensor_scalar(T.sofs[:, 16 * k + 4 * t:16 * k + 4 * t + 4], T.sofs[:, 16 * k:16 * k + 4], t, None, AluOpType.add))
-        return tok
-
-    need("v", LSEND)
-    k_g1 = picks(0)
-    need("v", LUN, k_base)
-    k_uo = done("vs", V.tensor_tensor(T.uo[:], T.lun[:], T.base[:], AluOpType.add))
-    picks(1)
-    k_g23 = picks(2)
-    need("v", k_uo)
-    k_s1 = places(0)
-
-    need("s", LB, k_g1)
-    k_bc1 = [done("ss", S.activation(T.bc1[:, 64 * t:64 * t + 64], T.bt[:, t:768].indirect(T.gofs[:, 0:4]), COPY)) for t in range(4)]
-    need("s", k_g23)
-    for t in range(4):
-        k_bc2 = done("ss", S.activation(T.bc2[:, t:512:4], T.bt[:, t:768].indirect(T.gofs[:, 4:12]), COPY))
-    k_bp = k_bp0
-    for u in range(2):
-        need("v", k_bp, k_s1, k_bc1[2 * u + 1])
-        k_bp = done("vs", V.tensor_copy(T.bp[:].indirect(T.sofs[:, 8 * u:8 * u + 8]), T.bc1[:, 128 * u:128 * u + 128]))
+        k_bc2 = done("ss", S.activation(T.bc2[:, t:640:4], T.bt[:, t:768].indirect(T.g2[:]), COPY))
+    need("v", k_bc1, k_bp0, k_ofs)
+    k_bp = done("vs", V.tensor_copy(T.bp[:, 0:W].indirect(places(first)), T.bc1[:]))
     need("v", k_bp)
     k_qb1 = done("vs", V.quantize_mx(T.qb1[:], T.sb1[:], T.bp[:]))
-    k_qa = []
-    for u, load in enumerate((LA0, LA1)):
-        need("v", load)
-        k_qa.append(done("vs", V.quantize_mx(T.qa[:, 256 * u:256 * u + 256], T.sa[:, 256 * u:256 * u + 256], T.at[:, 1024 * u:1024 * u + 1024])))
+
+    done("vs", V.tensor_scalar(T.bits[:, 2:3], T.pc[:], 2, 3, SHR, AND))
+    k_b = done("vs", V.tensor_scalar(T.bits[:, 3:4], T.pc[:], 3, None, AND))
+    k_mt = done("vs", V.memset(T.mt[:, 4 * UN:512], 0.0))
+    need("v", LA0)
+    k_qa0 = done("vs", V.quantize_mx(T.qa[:, 0:ABIG // 4], T.sa[:, 0:ABIG // 4], T.at[:, 0:ABIG]))
+    need("v", LA1)
+    k_qa1 = done("vs", V.quantize_mx(T.qa[:, ABIG // 4:512], T.sa[:, ABIG // 4:512], T.at[:, ABIG:2048]))
     need("v", k_bc2)
     k_qb2 = done("vs", V.quantize_mx(T.qb2[:], T.sb2[:], T.bc2[:]))
 
+    def product(out, i, n, codes, scales):
+        return done("ts", P.matmul_mx(out[:, 512 * i:512 * i + n], T.qa[:, 128 * i:128 * i + 128], T.sa[:, 128 * i:128 * i + 128], codes[:], scales[:], True, True))
+
     k_px, k_py = [], []
-    need("t", k_qb1)
+    need("t", k_qb1, k_qa0)
     for i in range(4):
-        need("t", k_qa[i // 2])
-        k_px.append(done("ts", P.matmul_mx(T.px[:, 512 * i:512 * i + 192], T.qa[:, 128 * i:128 * i + 128], T.sa[:, 128 * i:128 * i + 128], T.qb1[:], T.sb1[:], True, True)))
+        need("t", k_qa1 if i == 3 else k_qa0)
+        k_px.append(product(T.px, i, MINC, T.qb1, T.sb1))
     need("t", k_qb2)
     for i in range(4):
-        k_py.append(done("ts", P.matmul_mx(T.py[:, 512 * i:512 * i + 128], T.qa[:, 128 * i:128 * i + 128], T.sa[:, 128 * i:128 * i + 128], T.qb2[:], T.sb2[:], True, True)))
+        k_py.append(product(T.py, i, 160, T.qb2, T.sb2))
 
-    for i in (0, 2):
-        need("v", k_px[i])
-        k_c1v = done("vs", V.tensor_copy(T.h1[:, i:768:4], T.px[:, 512 * i:512 * i + 192]))
-    for i in (1, 3):
+    r0 = region(0)
+    for i in (0, 1):
         need("s", k_px[i])
-        k_c1s = done("ss", S.activation(T.h1[:, i:768:4], T.px[:, 512 * i:512 * i + 192], COPY))
-    need("v", k_c1v, k_c1s)
-    k_h1 = done("vs", V.quantize_mx(T.qh1[:], T.sh1[:], T.h1[:]))
-    k_zc = []
-    for k in range(2):
+        k_c0s = done("ss", S.activation(T.h[:, r0 + i:r0 + W:4], T.px[:, 512 * i:512 * i + SITE], COPY))
+    for i in (2, 3):
+        need("v", k_px[i])
+        k_c0v = done("vs", V.tensor_copy(T.h[:, r0 + i:r0 + W:4], T.px[:, 512 * i:512 * i + SITE]))
+    k_zc = {}
+    for k in range(1, 6):
+        c = 32 * compact.index(order[k])
         for t in range(4):
             need("s", k_py[t])
-            tok = done("ss", S.activation(T.zc[:, 256 * k + 64 * t:256 * k + 64 * t + 64], T.py[:, 512 * t + 64 * k:512 * t + 64 * k + 64], COPY))
-        k_zc.append(tok)
-    k_s2 = places(1)
-    k_s3 = places(2)
-    need("v", k_s2, k_h20, k_zc[0])
-    k_c2 = done("vs", V.tensor_copy(T.h2[:].indirect(T.sofs[:, 16:32]), T.zc[:, 0:256]))
-    need("v", k_c2)
-    k_h2 = done("vs", V.quantize_mx(T.qh2[:], T.sh2[:], T.h2[:]))
-    need("v", k_s3, k_h30, k_zc[1])
-    k_c3 = done("vs", V.tensor_copy(T.h3[:].indirect(T.sofs[:, 32:48]), T.zc[:, 256:512]))
-    need("v", k_c3)
-    k_h3 = done("vs", V.quantize_mx(T.qh3[:], T.sh3[:], T.h3[:]))
+            k_zc[k] = done("ss", S.activation(T.zc[:, 128 * (k - 1) + 32 * t:128 * (k - 1) + 32 * t + 32], T.py[:, 512 * t + c:512 * t + c + 32], COPY))
 
-    def bits(engines):
-        return sum(1 << e for e in engines)
+    def quantise(k):
+        return done("vs", V.quantize_mx(T.qh[:, MINC * k:MINC * k + MINC], T.sh[:, MINC * k:MINC * k + MINC], T.h[:, region(k):region(k) + 4 * MINC]))
 
-    def slot(receiver, sender):
-        return SLOT * (sender if sender < receiver else sender - 1)
+    need("v", k_c0v, k_c0s, k_pad)
+    k_h = [quantise(0)]
+    for k, zero in ((1, k_z1), (2, k_z3), (3, k_z3), (4, k_z5), (5, k_z5)):
+        need("v", zero, k_zc[k])
+        tok = done("vs", V.tensor_copy(T.h[:, region(k):region(k) + W].indirect(places(order[k])), T.zc[:, 128 * (k - 1):128 * k]))
+        need("v", tok)
+        k_h.append(quantise(k))
 
-    def transfer(x, engines, src, dst):
-        rid, pid = topo.addr(peers[x], core)
-        return RemoteDMATransfer(dst_ids=[DstId(rid=rid, pnc=pid)], dma_engine_mask=bits(engines), remote_sem=T.sem["arr%d" % me], srcs=[src], dsts=[dst])
+    def slot(k):
+        return UN + SITE * (4 - k)
+
+    def write(to, sem, at, n, codes, scales, lo):
+        rid, pid = topo.addr(to, core)
+        eng = topo.engines(core, to)
+        g.remote_dma(T.land[:, at:at + n].bitcast(dt.uint8), codes[:, lo:lo + n].bitcast(dt.uint8), sem, T.sem.sent, pid, rid, bits_of(eng))
+        g.remote_dma(T.lsc[:, at:at + n], scales[:, lo:lo + n], sem, T.sem.sent, pid, rid, bits_of(eng))
+        return 2 * len(eng)
 
     sent = 0
-    for k, (tok, qh, sh) in enumerate(((k_h1, T.qh1, T.sh1), (k_h2, T.qh2, T.sh2))):
-        need("g", tok)
-        for plane in range(2):
-            ts = []
-            for e in range(2):
-                x = 2 * groups[k] + e
-                eng = topo.engines(core, peers[x])
-                q = len(eng) // 4
-                part = 2 * ((k + plane) % 2) + e
-                at = slot(x, me)
-                if plane:
-                    src, dst = sh[:, SITE * e:SITE * e + SITE], T.lsc[:, at:at + SITE]
-                else:
-                    src, dst = qh[:, SITE * e:SITE * e + SITE].bitcast(dt.uint8), T.land[:, at:at + SITE].bitcast(dt.uint8)
-                ts.append(transfer(x, eng[q * part:q * part + q], src, dst))
-                sent += q
-            g.remote_dma_fused(ts, local_sem=T.sem.sent)
-    mate = me + 1 - 2 * odd
-    eng = topo.engines(core, peers[mate])
-    rid, pid = topo.addr(peers[mate], core)
-    at, lo = slot(mate, me), SITE * (1 - odd)
-    need("g", k_h3)
-    g.remote_dma(T.land[:, at:at + SITE].bitcast(dt.uint8), T.qh3[:, lo:lo + SITE].bitcast(dt.uint8), T.sem["arr%d" % me], T.sem.sent, pid, rid, bits(eng))
-    g.remote_dma(T.lsc[:, at:at + SITE], T.sh3[:, lo:lo + SITE], T.sem["arr%d" % me], T.sem.sent, pid, rid, bits(eng))
-    sent += 2 * len(eng)
-
-    k_zt = done("vs", V.memset(T.zt[:], 0.0))
-    need("v", k_zt)
     for k in range(5):
-        k_pad = done("vs", V.quantize_mx(T.land[:, SLOT * k + SITE:SLOT * (k + 1)], T.lsc[:, SLOT * k + SITE:SLOT * (k + 1)], T.zt[:]))
-    k_rpad = done("vs", V.quantize_mx(T.rl[:, UN:UN + 128], T.rs[:, UN:UN + 128], T.zt[:]))
+        need("g", k_h[k])
+        sent += write(peers[order[k]], T.sem["arr%d" % k], slot(k), SITE, T.qh, T.sh, MINC * k)
+    k_dump = done("gs", g.iota(T.dump[:], [[OC - UN, 2], [-16, 3]], -2 * OC, -1))
+    k_wv = done("gs", g.iota(T.wv[:], [[0, 2], [1, UN]], 0, 0, **FLT))
+    k_d0 = done("gs", g.iota(T.d0[:], [[0, OC // 2], [1000, 4]], 0, 0, **FLT))
 
     def decode(t, out, codes, scales, c, start, stop):
-        return done("ts", P.matmul_mx(out[:, 512 * t:512 * t + 128], T.qe[:, 128 * t:128 * t + 128], T.se[:, 128 * t:128 * t + 128], codes[:, c:c + 128], scales[:, c:c + 128], start, stop))
+        e = EAT + 128 * t
+        return done("ts", P.matmul_mx(out[:, 512 * t:512 * t + MINC], T.land[:, e:e + 128], T.lsc[:, e:e + 128], codes[:, c:c + MINC], scales[:, c:c + MINC], start, stop))
 
-    need("t", k_h3, k_e, k_c1v, k_c1s)
-    for t in range(4):
-        decode(t, T.px, T.qh3, T.sh3, SITE * odd, True, False)
-    need("t", k_pad)
-    n8 = len(eng)
-    first, second = (pair + 2) % 3, (pair + 1) % 3
-    for x, n in ((2 * first, n8 // 2), (2 * first + 1, n8 // 2), (2 * second, n8 // 2), (2 * second + 1, n8 // 2), (mate, 2 * n8)):
-        P.wait_ge(T.sem["arr%d" % x], n)
-        k_acc = [decode(t, T.px, T.land, T.lsc, slot(me, x), False, x == mate) for t in range(4)]
+    def arrivals(sender):
+        return 2 * len(topo.engines(sender, core))
 
-    k_mt = done("vs", V.memset(T.mt[:, 4 * UN:512], 0.0))
-    for t in range(4):
-        done("vs", V.memset(T.lf[:, SEC * t + UN:SEC * t + SEC], 0.0))
-        k_z0 = done("vs", V.memset(T.rf[:, SEC * t + UN:SEC * t + SEC], 0.0))
-    k_win = done("vs", V.memset(T.win[:], float(UN)))
-    k_d1 = done("vs", V.memset(T.d0[:], 1.0))
-    need("v", LUPL, k_jc, k_wv, k_mi)
-    k_ng = done("vs", V.tensor_scalar(T.neg[:], T.lupl[:], 0, None, AluOpType.is_lt))
-    k_mj = done("vs", V.tensor_scalar(T.mj[:], T.mi[:], 15, None, AluOpType.bitwise_and))
+    need("t", k_c0v, k_c0s, ("earr", arrivals(helper_of(core, T, topo))))
+    for k in (0, 1, 2, 5, 3, 4):
+        if k == 5:
+            need("t", k_h[5])
+            k_acc = [decode(t, T.px, T.qh, T.sh, MINC * 5, False, False) for t in range(4)]
+        else:
+            sender = [o for o in range(H) if o != me and stages(o, peers, topo)[k] == me][0]
+            need("t", ("arr%d" % k, arrivals(peers[sender])))
+            k_acc = [decode(t, T.px, T.land, T.lsc, slot(k), k == 0, k == 4) for t in range(4)]
+
+    need("v", LUPL, k_dump, k_b)
+    k_ng = done("vs", V.tensor_tensor(T.neg[:], T.lupl[:], T.dump[:], MULT))
+    k_win = done("vs", V.memset(T.win[:, 0:2 * OC], float(UN)))
     need("v", k_ng)
-    k_dp = done("vs", V.tensor_tensor(T.dump[:], T.neg[:], T.jc[:], AluOpType.mult))
-    k_d0 = done("vs", V.memset(T.d0[:, 0:192:16], 0.0))
-    need("v", k_dp)
-    k_uo2 = done("vs", V.tensor_tensor(T.uplo[:], T.lupl[:], T.dump[:], AluOpType.add))
-    k_mk = done("vs", V.tensor_scalar(T.mask[:], T.mj[:], 0, None, AluOpType.is_equal))
-    need("v", k_uo2)
+    k_uo = done("vs", V.tensor_tensor(T.uplo[:], T.neg[:], T.lupl[:], AluOpType.max))
+    done("vs", V.tensor_scalar(T.bitf[:, 2:3], T.bits[:, 2:3], 1000, None, MULT))
+    k_bf = done("vs", V.tensor_copy(T.bitf[:, 3:4], T.bits[:, 3:4]))
+    need("v", k_uo)
     for q in range(2):
-        k_uf = done("vs", V.tensor_copy(T.uofs[:, 4 * q:4 * q + 3], T.uplo[:, 3 * q:3 * q + 3]))
-    need("v", k_uf, k_win)
-    for q in range(2):
-        k_sc = done("vs", V.tensor_copy(T.win[:, WIN * q:WIN * q + WIN].indirect(T.uofs[:, 4 * q:4 * q + 3]), T.wv[:]))
-    need("v", k_sc, k_mk)
-    for q in range(2):
-        k_dm = done("vs", V.tensor_tensor(T.dm[:, 96 * q:96 * q + 96], T.win[:, WIN * q:WIN * q + 96], T.mask[:], AluOpType.mult))
-    need("v", k_dm, k_d0)
-    k_ds = done("vs", V.tensor_tensor_scan(T.ds[:], T.d0[:], T.dm[:], 0.0, AluOpType.mult, AluOpType.add))
-    need("v", k_ds)
-    k_io = done("vs", V.tensor_copy(T.iofs[:], T.ds[:, 15:192:16]))
+        k_uf = done("vs", V.tensor_scalar(T.uofs[:, 3 * q:3 * q + 3], T.uplo[:, 3 * q:3 * q + 3], OC * q, None, ADD))
+    done("vs", V.memset(T.lf[:, 4 * UN:4 * UN + 4], 0.0))
+    k_z0 = done("vs", V.memset(T.rf[:, 4 * UN:4 * UN + 4], 0.0))
+    need("v", k_uf, k_win, k_wv)
+    k_sc = done("vs", V.tensor_copy(T.win[:].indirect(T.uofs[:]), T.wv[:]))
 
-    far = UN * (1 - half)
+    far, near = UN * (1 - half), UN * half
     for t in (0, 2):
         need("v", k_acc[t])
         k_mv = done("vs", V.tensor_copy(T.mt[:, t:4 * UN:4], T.px[:, 512 * t + far:512 * t + far + UN]))
@@ -267,34 +278,40 @@ def rank_program(g, core, T, topo):
     need("v", k_mv, k_ms, k_mt)
     k_qm = done("vs", V.quantize_mx(T.qm[:], T.sm[:], T.mt[:]))
     other = T.cores[(rank + H) % (2 * H)]
-    rid, pid = topo.addr(other, core)
-    eng = topo.engines(core, other)
     need("g", k_qm)
-    g.remote_dma(T.rl[:, 0:UN].bitcast(dt.uint8), T.qm[:, 0:UN].bitcast(dt.uint8), T.sem.xarr, T.sem.sent, pid, rid, bits(eng))
-    g.remote_dma(T.rs[:, 0:UN], T.sm[:, 0:UN], T.sem.xarr, T.sem.sent, pid, rid, bits(eng))
-    sent += 2 * len(eng)
+    sent += write(other, T.sem.xarr, 0, UN, T.qm, T.sm, 0)
 
-    near = UN * half
-    need("s", k_mv, k_z0)
-    for t in range(4):
-        k_lf = done("ss", S.activation(T.lf[:, SEC * t:SEC * t + UN], T.px[:, 512 * t + near:512 * t + near + UN], COPY))
-    need("s", k_lf, k_io)
-    for t in range(4):
-        k_ya = done("ss", S.activation(T.yacc[:, t:384:4], T.lf[:, SEC * t:SEC * t + UN + 1].indirect(T.iofs[:, 6 * host:6 * host + 6]), COPY))
+    need("v", k_d0, k_bf)
+    k_mk = done("vs", V.tensor_scalar(T.mask[:], T.d0[:], T.bitf[:, 2:3], None, AluOpType.is_equal))
+    need("v", k_mk, k_sc)
+    k_dm = done("vs", V.tensor_tensor(T.dm[:], T.win[:, 0:2 * OC], T.mask[:], MULT))
+    need("v", k_dm)
+    k_ds = done("vs", V.tensor_tensor_scan(T.ds[:], T.d0[:], T.dm[:], 0.0, AluOpType.min, ADD))
+    need("v", k_ds)
+    k_io = {}
+    for q in (host, 1 - host):
+        k_io[q] = done("vs", V.tensor_scalar(T.iofs[:, 22 * q:22 * q + 21], T.ds[:, OC * q + 3:OC * q + OC:4], 4, T.bitf[:, 3:4], MULT, ADD))
 
-    need("t", k_zc[1], k_rpad)
-    P.wait_ge(T.sem.xarr, 2 * len(eng))
-    k_r = [decode(t, T.py, T.rl, T.rs, 0, True, True) for t in range(4)]
-    k_rf = []
-    for t in range(4):
+    for t in (1, 3, 0, 2):
+        if t == 0:
+            need("s", k_mv)
+        k_lf = done("ss", S.activation(T.lf[:, t:4 * UN:4], T.px[:, 512 * t + near:512 * t + near + UN], COPY))
+    need("s", k_lf, k_z0, k_io[host])
+    k_ya = done("ss", S.activation(T.yacc[:], T.lf[:].indirect(T.iofs[:, 22 * host:22 * host + 21]), COPY))
+
+    need("t", k_zc[5], ("xarr", arrivals(other)))
+    k_r = [decode(t, T.py, T.land, T.lsc, 0, True, True) for t in range(4)]
+    for t in (0, 2):
+        need("v", k_r[t])
+        k_rv = done("vs", V.tensor_copy(T.rf[:, t:4 * UN:4], T.py[:, 512 * t:512 * t + UN]))
+    for t in (1, 3):
         need("s", k_r[t])
-        k_rf.append(done("ss", S.activation(T.rf[:, SEC * t:SEC * t + UN], T.py[:, 512 * t:512 * t + UN], COPY)))
-    need("v", k_ya)
-    q = 6 * (1 - host)
-    for t in range(4):
-        need("v", k_rf[t])
-        k_yo = done("vs", V.tensor_tensor(T.yo[:, t:384:4], T.rf[:, SEC * t:SEC * t + UN + 1].indirect(T.iofs[:, q:q + 6]), T.yacc[:, t:384:4], AluOpType.add))
-    need("y", k_yo)
-    Y.dma_start(T.y[:], T.yo[:, 0:4 * OC]).then_inc(T.sem.stored, 16)
+        k_rs = done("ss", S.activation(T.rf[:, t:4 * UN:4], T.py[:, 512 * t:512 * t + UN], COPY))
+    need("v", k_rv, k_rs, k_ya, k_z0, k_io[1 - host])
+    q = 22 * (1 - host)
+    for lo, hi, queue in ((0, CUT, "y"), (CUT, 21, "s")):
+        tok = done("vs", V.tensor_tensor(T.yo[:, 16 * lo:16 * hi], T.rf[:].indirect(T.iofs[:, q + lo:q + hi]), T.yacc[:, 16 * lo:16 * hi], ADD))
+        need(queue, tok)
+        queues[queue].dma_start(T.y[:, 16 * lo:16 * hi], T.yo[:, 16 * lo:16 * hi]).then_inc(T.sem.stored, 16)
 
-    need("g", ("sent", sent), ("vs", count["vs"]), ("ss", count["ss"]), ("ts", count["ts"]), ("gs", count["gs"]), ("stored", 16))
+    need("g", ("sent", sent), ("vs", count["vs"]), ("ss", count["ss"]), ("ts", count["ts"]), ("gs", count["gs"]), ("stored", 32))

@@ -2,72 +2,87 @@ import numpy as np
 from concourse.bass import DstId, RemoteDMATransfer
 from concourse.mybir import dt, AluOpType, ActivationFunctionType
 
-UN, OC, H = 48, 84, 6
-SITE = 2 * UN
-W = 4 * SITE
+UN, OC, H, CAP = 48, 84, 6, 16
+TILE = UN + CAP
 MINC = 128
-EAT = UN + 5 * SITE
+ZAT = UN + 5 * TILE
+EAT = ZAT + TILE
 ABIG = 1536
 CUT = 10
+H0, H2, H1 = 192, 448, 960
+WD = 2 * OC
 
 F32, BF, I32, U16, X4, U8 = "float32", "bfloat16", "int32", "uint16", "float8_e4m3fn_x4", "uint8"
 SCRATCH = {
-    "lists": ("sbuf", [128, 24], I32), "lupl": ("sbuf", [128, 6], I32),
-    "pc": ("sbuf", [128, 1], I32), "bits": ("sbuf", [128, 4], I32), "bitf": ("sbuf", [128, 4], F32),
-    "colb": ("sbuf", [128, 4], I32), "cof": ("sbuf", [128, 4], U16),
-    "kk": ("sbuf", [128, 64], F32), "k4": ("sbuf", [128, 64], F32),
-    "off": ("sbuf", [128, 64], F32), "ofs": ("sbuf", [128, 64], U16), "g2": ("sbuf", [128, 10], U16),
+    "lists": ("sbuf", [128, 24], I32), "late": ("sbuf", [128, 12], I32),
+    "ofs": ("sbuf", [128, 96], U16), "g2": ("sbuf", [128, 10], U16), "e01": ("sbuf", [128, 6], I32),
+    "e80": ("sbuf", [128, 6], I32), "ue": ("sbuf", [128, 6], I32), "sofs": ("sbuf", [128, 16], U16),
+    "p8": ("sbuf", [128, 6], I32), "pe": ("sbuf", [128, 6], I32), "pofs": ("sbuf", [128, 24], U16),
     "bt": ("sbuf", [128, 768], BF), "at": ("sbuf", [128, 2048], BF),
-    "bc1": ("sbuf", [128, 128], BF), "bp": ("sbuf", [128, 512], BF), "bc2": ("sbuf", [128, 640], BF),
+    "bc1": ("sbuf", [128, 128], BF), "bp": ("sbuf", [128, 512], BF), "bc2": ("sbuf", [128, 512], BF), "bo": ("sbuf", [128, 512], BF),
     "qa": ("sbuf", [128, 512], X4), "sa": ("sbuf", [128, 512], U8),
     "qb1": ("sbuf", [128, 128], X4), "sb1": ("sbuf", [128, 128], U8),
-    "qb2": ("sbuf", [128, 160], X4), "sb2": ("sbuf", [128, 160], U8),
-    "ones": ("sbuf", [128, 520], BF), "strip": ("sbuf", [128, 520], BF),
-    "qe": ("sbuf", [128, 512], X4), "se": ("sbuf", [128, 512], U8),
-    "zc": ("sbuf", [128, 640], BF), "h": ("sbuf", [128, 6 * W + 128], BF),
-    "qh": ("sbuf", [128, 6 * MINC], X4), "sh": ("sbuf", [128, 6 * MINC], U8),
+    "qb2": ("sbuf", [128, 128], X4), "sb2": ("sbuf", [128, 128], U8),
+    "qbo": ("sbuf", [128, 128], X4), "sbo": ("sbuf", [128, 128], U8),
+    "ones": ("sbuf", [128, 520], BF), "strip": ("sbuf", [128, 520], BF), "zt": ("sbuf", [128, 512], BF),
+    "wt": ("sbuf", [128, 2 * 512], BF),
+    "qe": ("sbuf", [128, TILE + 512], X4), "se": ("sbuf", [128, TILE + 512], U8),
+    "qw": ("sbuf", [128, 256], X4), "sw": ("sbuf", [128, 256], U8),
+    "zc": ("sbuf", [128, 256], BF), "h": ("sbuf", [128, H1 + 512], BF),
+    "qh": ("sbuf", [128, 3 * MINC], X4), "sh": ("sbuf", [128, 3 * MINC], U8),
     "land": ("sbuf", [128, EAT + 512], X4), "lsc": ("sbuf", [128, EAT + 512], U8),
-    "mt": ("sbuf", [128, 512], BF), "qm": ("sbuf", [128, 128], X4), "sm": ("sbuf", [128, 128], U8),
-    "lf": ("sbuf", [128, 4 * UN + 4], F32), "rf": ("sbuf", [128, 4 * UN + 4], F32),
-    "yacc": ("sbuf", [128, 4 * OC], F32), "yo": ("sbuf", [128, 4 * OC], F32),
-    "dump": ("sbuf", [128, 6], I32), "neg": ("sbuf", [128, 6], I32), "uplo": ("sbuf", [128, 6], I32),
-    "uofs": ("sbuf", [128, 6], U16), "wv": ("sbuf", [128, SITE], F32), "win": ("sbuf", [128, 376], F32),
-    "d0": ("sbuf", [128, 2 * OC], F32), "mask": ("sbuf", [128, 2 * OC], F32), "dm": ("sbuf", [128, 2 * OC], F32),
-    "ds": ("sbuf", [128, 2 * OC], F32), "iofs": ("sbuf", [128, 44], U16),
+    "fold": ("sbuf", [128, 4 * UN], F32), "qm": ("sbuf", [128, 128], X4), "sm": ("sbuf", [128, 128], U8),
+    "zn": ("sbuf", [128, H * 64], BF), "nt": ("sbuf", [128, 12 * WD], BF),
+    "qn": ("sbuf", [128, 3 * WD], X4), "sn": ("sbuf", [128, 3 * WD], U8),
+    "rf": ("sbuf", [128, 4 * UN + 4], F32), "yacc": ("sbuf", [128, 4 * OC], F32), "yo": ("sbuf", [128, 4 * OC], F32),
+    "pc": ("sbuf", [128, 1], I32), "bits": ("sbuf", [128, 4], I32), "bitf": ("sbuf", [128, 4], F32),
+    "dump": ("sbuf", [128, 3], I32), "neg": ("sbuf", [128, 3], I32), "uplo": ("sbuf", [128, 3], I32),
+    "uofs": ("sbuf", [128, 4], U16), "wv": ("sbuf", [128, UN], F32), "win": ("sbuf", [128, 260], F32),
+    "d0": ("sbuf", [128, OC], F32), "mask": ("sbuf", [128, OC], F32), "dm": ("sbuf", [128, OC], F32),
+    "ds": ("sbuf", [128, OC], F32), "iofs": ("sbuf", [128, 22], U16),
     "px": ("psum", [128, 2048], F32), "py": ("psum", [128, 2048], F32),
 }
-SEMAPHORES = ["gs", "vs", "ss", "ts", "ldl", "ldupl", "ldb", "lda0", "lda1", "stored", "sent", "xarr", "earr"] + ["arr%d" % k for k in range(5)]
+SEMAPHORES = ["gs", "vs", "ss", "ts", "ldl", "ldlate", "ldb", "lda0", "lda1", "stored", "sent", "xarr", "earr", "warr"] + ["arr%d" % k for k in range(5)]
 
 
 def helper_of(c, T, topo):
     return min(o for o in topo.cores_of(c) if o not in T.cores and topo.die(o) == topo.die(c))
 
 
-def stages(x, peers, topo):
-    ring = [(x + s) % H for s in range(1, H)]
-    mate = [o for o in ring if topo.mates(peers[x], peers[o])]
-    plane = [o for o in ring if topo.same_plane(peers[x], peers[o])]
-    return [o for o in ring if o not in mate + plane] + plane + mate
-
-
 def bits_of(engines):
     return sum(1 << e for e in engines)
 
 
+def tile_at(j):
+    return UN + TILE * j
+
+
 def helper_program(g, core, target, T, topo):
     V = g.vector
-    V.memset(T.ones[:], 1.0).then_inc(T.sem.vs, 1)
-    g.wait_ge(T.sem.vs, 1)
-    g.affine_select(T.strip[:], T.ones[:], [[1, 520]], AluOpType.is_equal, 0.0, -4, -4).then_inc(T.sem.gs, 1)
-    V.wait_ge(T.sem.gs, 1)
-    for t in range(4):
-        V.quantize_mx(T.qe[:, 128 * t:128 * t + 128], T.se[:, 128 * t:128 * t + 128], T.strip[:, 4 - t:516 - t]).then_inc(T.sem.vs, 1)
-    g.wait_ge(T.sem.vs, 5)
     rid, pid = topo.addr(target, core)
     eng = topo.engines(core, target)
-    g.remote_dma(T.land[:, EAT:EAT + 512].bitcast(dt.uint8), T.qe[:].bitcast(dt.uint8), T.sem.earr, T.sem.sent, pid, rid, bits_of(eng))
-    g.remote_dma(T.lsc[:, EAT:EAT + 512], T.se[:], T.sem.earr, T.sem.sent, pid, rid, bits_of(eng))
-    g.wait_ge(T.sem.sent, 2 * len(eng))
+    V.memset(T.ones[:], 1.0).then_inc(T.sem.vs, 1)
+    V.memset(T.zt[:], 0.0).then_inc(T.sem.vs, 1)
+    g.wait_ge(T.sem.vs, 1)
+    g.affine_select(T.strip[:], T.ones[:], [[1, 520]], AluOpType.is_equal, 0.0, -4, -4).then_inc(T.sem.gs, 1)
+    V.wait_ge(T.sem.vs, 2)
+    V.quantize_mx(T.qe[:, 0:MINC], T.se[:, 0:MINC], T.zt[:]).then_inc(T.sem.vs, 1)
+    V.wait_ge(T.sem.gs, 1)
+    V.wait_ge(T.sem.vs, 3)
+    for t in range(4):
+        c = TILE + 128 * t
+        V.quantize_mx(T.qe[:, c:c + 128], T.se[:, c:c + 128], T.strip[:, 4 - t:516 - t]).then_inc(T.sem.vs, 1)
+    g.wait_ge(T.sem.vs, 7)
+    g.remote_dma(T.land[:, ZAT:EAT + 512].bitcast(dt.uint8), T.qe[:].bitcast(dt.uint8), T.sem.earr, T.sem.sent, pid, rid, bits_of(eng))
+    g.remote_dma(T.lsc[:, ZAT:EAT + 512], T.se[:], T.sem.earr, T.sem.sent, pid, rid, bits_of(eng))
+    for u in range(2):
+        V.tensor_tensor(T.wt[:, 512 * u:512 * u + 512], T.strip[:, 4 - 2 * u:516 - 2 * u], T.strip[:, 3 - 2 * u:515 - 2 * u], AluOpType.add).then_inc(T.sem.vs, 1)
+    V.wait_ge(T.sem.vs, 9)
+    V.quantize_mx(T.qw[:], T.sw[:], T.wt[:]).then_inc(T.sem.vs, 1)
+    g.wait_ge(T.sem.vs, 10)
+    g.remote_dma(T.qw[:].bitcast(dt.uint8), T.qw[:].bitcast(dt.uint8), T.sem.warr, T.sem.sent, pid, rid, bits_of(eng))
+    g.remote_dma(T.sw[:], T.sw[:], T.sem.warr, T.sem.sent, pid, rid, bits_of(eng))
+    g.wait_ge(T.sem.sent, 4 * len(eng))
     g.wait_ge(T.sem.gs, 1)
 
 
@@ -85,9 +100,14 @@ def rank_program(g, core, T, topo):
     half, me = rank // H, rank % H
     peers = [T.cores[half * H + x] for x in range(H)]
     host = topo.host(core)
-    order = stages(me, peers, topo) + [me]
-    first = order[0]
-    compact = [x for x in range(H) if x != first]
+    helper = helper_of(core, T, topo)
+    mate = [x for x in range(H) if topo.mates(core, peers[x])][0]
+    lows = [x for x in range(H) if x + 1 < H and topo.mates(peers[x], peers[x + 1])]
+    pair = lows.index(min(me, mate))
+    ahead = [lows[(pair + s) % 3] for s in (1, 2)]
+    behind = [lows[(pair - s) % 3] for s in (1, 2)]
+    NEAR, FAR = H * half, H * (1 - half)
+    low = me < mate
 
     count = {"gs": 0, "vs": 0, "ss": 0, "ts": 0}
     queues = {"g": g, "v": V, "s": S, "t": P, "y": Y}
@@ -107,211 +127,269 @@ def rank_program(g, core, T, topo):
                 queues[q].wait_ge(T.sem[sem], n)
                 known[q][sem] = n
 
+    def copy(q, out, in_):
+        return done("vs", V.tensor_copy(out, in_)) if q == "v" else done("ss", S.activation(out, in_, COPY))
+
+    def scalar(out, in_, *rest):
+        return done("vs", V.tensor_scalar(out, in_, *rest))
+
+    def quantise(codes, scales, tile):
+        return done("vs", V.quantize_mx(codes, scales, tile))
+
+    def zero(out, n):
+        return done("ss", S.activation(out, T.bt[:, 0:n], COPY, scale=0.0))
+
     for k in range(2):
         Y.dma_start(T.lists[16 * k:16 * k + 16, 0:12], T.send[:]).then_inc(T.sem.ldl, 16)
         S.dma_start(T.lists[16 * k:16 * k + 16, 12:24], T.un[:]).then_inc(T.sem.ldl, 16)
     Y.dma_start(T.bt[:], T.b[:]).then_inc(T.sem.ldb, 16)
     Y.dma_start(T.at[:, 0:ABIG], T.a[:, 0:ABIG]).then_inc(T.sem.lda0, 16)
     Y.dma_start(T.at[:, ABIG:2048], T.a[:, ABIG:2048]).then_inc(T.sem.lda1, 16)
-    for k in range(8):
-        Y.dma_start(T.lupl[16 * k:16 * k + 16, :], T.upl[:]).then_inc(T.sem.ldupl, 16)
-    LL, LUPL, LB, LA0, LA1 = ("ldl", 64), ("ldupl", 128), ("ldb", 16), ("lda0", 16), ("lda1", 16)
+    for k in range(2):
+        Y.dma_start(T.late[16 * k:16 * k + 16, 0:H], T.place[:, NEAR:NEAR + H]).then_inc(T.sem.ldlate, 16)
+        Y.dma_start(T.late[16 * k:16 * k + 16, H:2 * H], T.upl[:]).then_inc(T.sem.ldlate, 16)
+    LL, LATE, LB, LA0, LA1 = ("ldl", 64), ("ldlate", 64), ("ldb", 16), ("lda0", 16), ("lda1", 16)
 
+    k_zh2 = done("gs", g.iota(T.h[:, H2:H2 + 512], [[0, 512]], 0, 0, **FLT))
+    k_e80 = done("gs", g.iota(T.e80[:], [[0, 3], [TILE + CAP, 2]], 0, 0))
     k_pc = done("gs", g.iota(T.pc[:], [[0, 1]], 0, 1))
-    done("gs", g.iota(T.colb[:, 0:1], [[0, 1]], 2 * (first // 2), 0))
-    k_colb = done("gs", g.iota(T.colb[:, 1:4], [[2, 3]], 12, 0))
-    done("gs", g.iota(T.kk[:, 0:16], [[0, 2], [1, 4], [0, 2]], 0, 0, **FLT))
-    k_kk = done("gs", g.iota(T.kk[:, 16:64], [[0, 6], [1, 4], [4 * UN, 2]], 0, 0, **FLT))
-
-    def region(k):
-        return W * (5 - k)
-
-    k_z1 = done("gs", g.iota(T.h[:, region(1):region(0)], [[0, W]], 0, 0, **FLT))
-    k_z3 = done("gs", g.iota(T.h[:, region(3):region(1)], [[0, 2 * W]], 0, 0, **FLT))
-
+    k_e01 = done("gs", g.iota(T.e01[:], [[0, 3], [1, 2]], 0, 0))
+    k_dump = done("gs", g.iota(T.dump[:], [[-16, 3]], -OC, -1))
+    k_wv = done("gs", g.iota(T.wv[:], [[1, UN]], 0, 0, **FLT))
+    k_d0 = done("gs", g.iota(T.d0[:], [[0, OC // 4], [1000, 4]], 0, 0, **FLT))
     k_bp0 = done("vs", V.memset(T.bp[:], 0.0))
-    need("v", k_pc)
-    done("vs", V.tensor_scalar(T.bits[:, 0:1], T.pc[:], 1, None, AND))
-    k_b = done("vs", V.tensor_scalar(T.bits[:, 1:2], T.pc[:], 3, 1, SHR, AND))
-    k_pad = done("vs", V.memset(T.h[:, 6 * W:6 * W + 128], 0.0))
-    need("v", k_b)
-    done("vs", V.tensor_scalar(T.bitf[:, 0:1], T.bits[:, 0:1], H, None, MULT))
-    k_b = done("vs", V.tensor_copy(T.bitf[:, 1:2], T.bits[:, 1:2]))
-    need("v", k_b, k_colb)
-    k_cof = done("vs", V.tensor_scalar(T.cof[:], T.colb[:], T.bitf[:, 0:1], T.bitf[:, 1:2], ADD, ADD))
-    need("v", k_kk)
-    k_k4 = done("vs", V.tensor_scalar(T.k4[:], T.kk[:], 0.25, None, MULT))
+    k_zbo = done("vs", V.memset(T.bo[:], 0.0))
+    k_z0 = done("vs", V.memset(T.rf[:, 4 * UN:4 * UN + 4], 0.0))
+    k_win = done("vs", V.memset(T.win[:, 0:OC], float(UN)))
     need("s", k_bp0)
-    for k in (4, 5):
-        k_z5 = done("ss", S.activation(T.h[:, region(k):region(k) + W], T.bp[:, 0:W], COPY))
+    k_zh1 = copy("s", T.h[:, H1:H1 + 512], T.bp[:])
 
     need("v", LL)
     for p0 in (32, 64, 96):
-        k_l = done("vs", V.tensor_copy(T.lists[p0:p0 + 32, :], T.lists[0:32, :]))
-    need("v", k_l, k_cof, k_k4)
-    k_off = done("vs", V.tensor_tensor(T.off[:], T.lists[:].indirect(T.cof[:]), T.k4[:], ADD))
-    need("v", k_off)
-    k_ofs = done("vs", V.tensor_scalar(T.ofs[:], T.off[:], 4, None, MULT))
-    for h in range(2):
-        if first > 0:
-            k_g2 = done("vs", V.tensor_scalar(T.g2[:, h:2 * first:2], T.lists[:, H * h:H * h + first], 4, None, MULT))
-        if first < H - 1:
-            k_g2 = done("vs", V.tensor_scalar(T.g2[:, 2 * first + h:10:2], T.lists[:, H * h + first + 1:H * h + H], 4, None, MULT))
+        k_l = copy("v", T.lists[p0:p0 + 32, :], T.lists[0:32, :])
+    need("v", k_l)
+    for s, x in enumerate(ahead):
+        for i, c in enumerate((FAR, NEAR)):
+            k_g2 = scalar(T.g2[:, 4 * s + 2 * i:4 * s + 2 * i + 2], T.lists[:, c + x:c + x + 2], 4, None, MULT)
+    for t in range(4):
+        k_ofs = scalar(T.ofs[:, t:96:4], T.lists[:], 4, t, MULT, ADD)
+    c = NEAR + lows[pair]
+    k_g1 = scalar(T.g2[:, 8:10], T.lists[:, c:c + 2], 4, None, MULT)
 
-    def places(x):
-        return T.ofs[:, 16 + 8 * x:24 + 8 * x]
+    def picks(c):
+        return T.ofs[:, 4 * c:4 * c + 4]
 
-    need("s", LB, k_ofs)
-    k_bc1 = done("ss", S.activation(T.bc1[:], T.bt[:].indirect(T.ofs[:, 8 * (first % 2):8 * (first % 2) + 8]), COPY))
+    def places(c):
+        return T.ofs[:, 48 + 4 * c:52 + 4 * c]
+
+    f0, n0, t0, o0 = (2 * CAP, 0, CAP, 0) if low else (0, UN, 0, TILE)
+    need("s", LB, k_zh1, k_g1)
+    for t in range(4):
+        k_bn = copy("s", T.bp[:, 4 * n0 + t:4 * n0 + 128:4], T.bt[:, t:768].indirect(T.g2[:, 8:10]))
     need("s", k_g2)
     for t in range(4):
-        k_bc2 = done("ss", S.activation(T.bc2[:, t:640:4], T.bt[:, t:768].indirect(T.g2[:]), COPY))
-    need("v", k_bc1, k_bp0, k_ofs)
-    k_bp = done("vs", V.tensor_copy(T.bp[:, 0:W].indirect(places(first)), T.bc1[:]))
-    need("v", k_bp)
-    k_qb1 = done("vs", V.quantize_mx(T.qb1[:], T.sb1[:], T.bp[:]))
+        k_bc2 = copy("s", T.bc2[:, t:512:4], T.bt[:, t:768].indirect(T.g2[:, 0:8]))
+    need("v", LB, k_ofs)
+    k_bc1 = copy("v", T.bc1[:, 0:64], T.bt[:].indirect(picks(FAR + mate)))
+    need("v", k_e80)
+    k_ue = done("vs", V.tensor_tensor(T.ue[:], T.lists[:, 12 + FAR:12 + FAR + H], T.e80[:], ADD))
+    need("v", k_bc1, k_bp0, k_zh1)
+    k_bp = copy("v", T.bp[:, 4 * f0:4 * (f0 + UN)].indirect(places(FAR + mate)), T.bc1[:, 0:64])
 
-    done("vs", V.tensor_scalar(T.bits[:, 2:3], T.pc[:], 2, 3, SHR, AND))
-    k_b = done("vs", V.tensor_scalar(T.bits[:, 3:4], T.pc[:], 3, None, AND))
-    k_mt = done("vs", V.memset(T.mt[:, 4 * UN:512], 0.0))
-    need("v", LA0)
-    k_qa0 = done("vs", V.quantize_mx(T.qa[:, 0:ABIG // 4], T.sa[:, 0:ABIG // 4], T.at[:, 0:ABIG]))
-    need("v", LA1)
-    k_qa1 = done("vs", V.quantize_mx(T.qa[:, ABIG // 4:512], T.sa[:, ABIG // 4:512], T.at[:, ABIG:2048]))
-    need("v", k_bc2)
-    k_qb2 = done("vs", V.quantize_mx(T.qb2[:], T.sb2[:], T.bc2[:]))
-
-    def product(out, i, n, codes, scales):
-        return done("ts", P.matmul_mx(out[:, 512 * i:512 * i + n], T.qa[:, 128 * i:128 * i + 128], T.sa[:, 128 * i:128 * i + 128], codes[:], scales[:], True, True))
-
-    k_px, k_py = [], []
-    need("t", k_qb1, k_qa0)
-    for i in range(4):
-        need("t", k_qa1 if i == 3 else k_qa0)
-        k_px.append(product(T.px, i, MINC, T.qb1, T.sb1))
-    need("t", k_qb2)
-    for i in range(4):
-        k_py.append(product(T.py, i, 160, T.qb2, T.sb2))
-
-    r0 = region(0)
-    for i in (0, 1):
-        need("s", k_px[i])
-        k_c0s = done("ss", S.activation(T.h[:, r0 + i:r0 + W:4], T.px[:, 512 * i:512 * i + SITE], COPY))
-    for i in (2, 3):
-        need("v", k_px[i])
-        k_c0v = done("vs", V.tensor_copy(T.h[:, r0 + i:r0 + W:4], T.px[:, 512 * i:512 * i + SITE]))
-    k_zc = {}
-    for k in range(1, 6):
-        c = 32 * compact.index(order[k])
+    def pair_places(s):
         for t in range(4):
-            need("s", k_py[t])
-            k_zc[k] = done("ss", S.activation(T.zc[:, 128 * (k - 1) + 32 * t:128 * (k - 1) + 32 * t + 32], T.py[:, 512 * t + c:512 * t + c + 32], COPY))
+            tok = scalar(T.sofs[:, 8 * s + 2 * t:8 * s + 2 * t + 2], T.ue[:, ahead[s]:ahead[s] + 2], 4, t, MULT, ADD)
+        return tok
 
-    def quantise(k):
-        return done("vs", V.quantize_mx(T.qh[:, MINC * k:MINC * k + MINC], T.sh[:, MINC * k:MINC * k + MINC], T.h[:, region(k):region(k) + 4 * MINC]))
+    need("v", k_ue)
+    k_so = [pair_places(0)]
+    need("v", LA0)
+    k_qa0 = quantise(T.qa[:, 0:ABIG // 4], T.sa[:, 0:ABIG // 4], T.at[:, 0:ABIG])
+    need("v", k_bp, k_bn)
+    k_qb1 = quantise(T.qb1[:], T.sb1[:], T.bp[:])
+    need("v", LA1)
+    k_qa1 = quantise(T.qa[:, ABIG // 4:512], T.sa[:, ABIG // 4:512], T.at[:, ABIG:2048])
+    need("v", k_bc2)
+    k_qb2 = quantise(T.qb2[:], T.sb2[:], T.bc2[:])
 
-    need("v", k_c0v, k_c0s, k_pad)
-    k_h = [quantise(0)]
-    for k, zero in ((1, k_z1), (2, k_z3), (3, k_z3), (4, k_z5), (5, k_z5)):
-        need("v", zero, k_zc[k])
-        tok = done("vs", V.tensor_copy(T.h[:, region(k):region(k) + W].indirect(places(order[k])), T.zc[:, 128 * (k - 1):128 * k]))
-        need("v", tok)
-        k_h.append(quantise(k))
+    def product(out, i, codes, scales, start, stop):
+        return done("ts", P.matmul_mx(out[:, 512 * i:512 * i + MINC], T.qa[:, 128 * i:128 * i + 128], T.sa[:, 128 * i:128 * i + 128],
+                                      codes[:], scales[:], start, stop))
 
-    def slot(k):
-        return UN + SITE * (4 - k)
+    for i in range(4):
+        need("t", k_qb1, k_qa1 if i == 3 else k_qa0)
+        need("v", product(T.px, i, T.qb1, T.sb1, True, True))
+        k_c0 = copy("v", T.h[:, H0 + i:H0 + 4 * TILE:4], T.px[:, 512 * i + t0:512 * i + t0 + TILE])
+    need("t", k_qb2)
+    k_py = [product(T.py, i, T.qb2, T.sb2, True, True) for i in range(4)]
+    need("v", k_c0, k_zh2)
+    k_h = [quantise(T.qh[:, 0:MINC], T.sh[:, 0:MINC], T.h[:, H0:H0 + 512])]
 
-    def write(to, sem, at, n, codes, scales, lo):
+    def near_cast(qs, x, bank, c, toks):
+        out = {}
+        for t, q in enumerate(qs):
+            if q != ".":
+                need(q, toks[t])
+                out[q] = copy(q, T.zn[:, 64 * x + 16 * t:64 * x + 16 * t + 16], bank[:, 512 * t + c:512 * t + c + CAP])
+        return list(out.values())
+
+    def pair_cast(q, s, t, tok):
+        c, at = 512 * t + 64 * s, (H1, H2)[s] + 4 * UN
+        need(q, tok, k_zh1, k_zh2, *k_h[:s])
+        copy(q, T.zc[:, 128 * s + 32 * t:128 * s + 32 * t + 32], T.py[:, c:c + 32])
+        return copy(q, T.h[:, at + t:at + 128:4], T.py[:, c + 32:c + 64])
+
+    k_first = [pair_cast("s", 0, t, k_py[t]) for t in range(4)]
+    k_second = [pair_cast("s", 1, t, k_py[t]) for t in range(4)]
+    for s, (at, toks) in enumerate(((H1, k_first), (H2, k_second))):
+        if s == 0:
+            k_so.append(pair_places(1))
+        need("v", k_so[s], *toks)
+        need("v", copy("v", T.h[:, at:at + 512].indirect(T.sofs[:, 8 * s:8 * s + 8]), T.zc[:, 128 * s:128 * s + 128]))
+        k_h.append(quantise(T.qh[:, MINC * (s + 1):MINC * (s + 2)], T.sh[:, MINC * (s + 1):MINC * (s + 2)], T.h[:, at:at + 512]))
+
+    def write(to, sem, at, n, codes, scales):
         rid, pid = topo.addr(to, core)
         eng = topo.engines(core, to)
-        g.remote_dma(T.land[:, at:at + n].bitcast(dt.uint8), codes[:, lo:lo + n].bitcast(dt.uint8), sem, T.sem.sent, pid, rid, bits_of(eng))
-        g.remote_dma(T.lsc[:, at:at + n], scales[:, lo:lo + n], sem, T.sem.sent, pid, rid, bits_of(eng))
+        g.remote_dma(T.land[:, at:at + n].bitcast(dt.uint8), codes[:, 0:n].bitcast(dt.uint8), sem, T.sem.sent, pid, rid, bits_of(eng))
+        g.remote_dma(T.lsc[:, at:at + n], scales[:, 0:n], sem, T.sem.sent, pid, rid, bits_of(eng))
         return 2 * len(eng)
 
-    sent = 0
-    for k in range(5):
-        need("g", k_h[k])
-        sent += write(peers[order[k]], T.sem["arr%d" % k], slot(k), SITE, T.qh, T.sh, MINC * k)
-    k_dump = done("gs", g.iota(T.dump[:], [[OC - UN, 2], [-16, 3]], -2 * OC, -1))
-    k_wv = done("gs", g.iota(T.wv[:], [[0, 2], [1, UN]], 0, 0, **FLT))
-    k_d0 = done("gs", g.iota(T.d0[:], [[0, OC // 2], [1000, 4]], 0, 0, **FLT))
+    need("g", k_h[0])
+    sent = write(peers[mate], T.sem.arr4, tile_at(4), TILE, T.qh, T.sh)
+    for s, x in enumerate(ahead):
+        need("g", k_h[s + 1])
+        j = 2 * (1 - s) + (0 if low else 1)
+        for plane in range(2):
+            ts = []
+            for e in range(2):
+                rid, pid = topo.addr(peers[x + e], core)
+                eng = topo.engines(core, peers[x + e])
+                n, lo = len(eng) // 2, MINC * (s + 1) + TILE * e
+                if plane:
+                    src, dst = T.sh[:, lo:lo + TILE], T.lsc[:, tile_at(j):tile_at(j) + TILE]
+                else:
+                    src, dst = T.qh[:, lo:lo + TILE].bitcast(dt.uint8), T.land[:, tile_at(j):tile_at(j) + TILE].bitcast(dt.uint8)
+                ts.append(RemoteDMATransfer(dst_ids=[DstId(rid=rid, pnc=pid)], dma_engine_mask=bits_of(eng[n * e:n * e + n]),
+                                            remote_sem=T.sem["arr%d" % j], srcs=[src], dsts=[dst]))
+                sent += n
+            g.remote_dma_fused(ts, local_sem=T.sem.sent)
 
-    def decode(t, out, codes, scales, c, start, stop):
-        e = EAT + 128 * t
-        return done("ts", P.matmul_mx(out[:, 512 * t:512 * t + MINC], T.land[:, e:e + 128], T.lsc[:, e:e + 128], codes[:, c:c + MINC], scales[:, c:c + MINC], start, stop))
+    k_bco = copy("s", T.bc1[:, 64:128], T.bt[:].indirect(picks(FAR + me)))
+    k_own = near_cast("ssss", me, T.px, o0, [k_c0] * 4)
+    k_zn = [zero(T.nt[:, 4 * WD * k:4 * WD * (k + 1)], 4 * WD) for k in range(2)]
+    k_zn.append(done("gs", g.iota(T.nt[:, 8 * WD:12 * WD], [[0, 4 * WD]], 0, 0, **FLT)))
+    need("v", k_bco, k_zbo)
+    k_bo = copy("v", T.bo[:, 0:4 * UN].indirect(places(FAR + me)), T.bc1[:, 64:128])
+    need("v", LATE)
+    for p0 in (32, 64, 96):
+        k_l = copy("v", T.late[p0:p0 + 32, :], T.late[0:32, :])
+    need("v", k_bo)
+    k_qbo = quantise(T.qbo[:], T.sbo[:], T.bo[:])
 
-    def arrivals(sender):
-        return 2 * len(topo.engines(sender, core))
-
-    need("t", k_c0v, k_c0s, ("earr", arrivals(helper_of(core, T, topo))))
-    for k in (0, 1, 2, 5, 3, 4):
-        if k == 5:
-            need("t", k_h[5])
-            k_acc = [decode(t, T.px, T.qh, T.sh, MINC * 5, False, False) for t in range(4)]
-        else:
-            sender = [o for o in range(H) if o != me and stages(o, peers, topo)[k] == me][0]
-            need("t", ("arr%d" % k, arrivals(peers[sender])))
-            k_acc = [decode(t, T.px, T.land, T.lsc, slot(k), k == 0, k == 4) for t in range(4)]
-
-    need("v", LUPL, k_dump, k_b)
-    k_ng = done("vs", V.tensor_tensor(T.neg[:], T.lupl[:], T.dump[:], MULT))
-    k_win = done("vs", V.memset(T.win[:, 0:2 * OC], float(UN)))
+    q = H + 3 * (1 - host)
+    need("v", k_l, k_dump)
+    k_p8 = scalar(T.p8[:], T.late[:, 0:H], 8, None, MULT)
+    k_ng = done("vs", V.tensor_tensor(T.neg[:], T.late[:, q:q + 3], T.dump[:], MULT))
+    need("v", k_p8, k_e01)
+    k_pe = done("vs", V.tensor_tensor(T.pe[:], T.p8[:], T.e01[:], ADD))
     need("v", k_ng)
-    k_uo = done("vs", V.tensor_tensor(T.uplo[:], T.neg[:], T.lupl[:], AluOpType.max))
-    done("vs", V.tensor_scalar(T.bitf[:, 2:3], T.bits[:, 2:3], 1000, None, MULT))
-    k_bf = done("vs", V.tensor_copy(T.bitf[:, 3:4], T.bits[:, 3:4]))
+    k_uo = done("vs", V.tensor_tensor(T.uplo[:], T.neg[:], T.late[:, q:q + 3], AluOpType.max))
+    need("v", k_pc)
+    for c, (shift, mask) in enumerate(((2, 3), (0, 3))):
+        k_b = scalar(T.bits[:, c:c + 1], T.pc[:], shift, mask, SHR, AND)
+    need("v", k_pe)
+    for t in range(4):
+        k_po = scalar(T.pofs[:, t:24:4], T.pe[:], 2 * t, None, ADD)
+    need("v", k_b)
+    scalar(T.bitf[:, 0:1], T.bits[:, 0:1], 1000, None, MULT)
+    k_bf = copy("v", T.bitf[:, 1:2], T.bits[:, 1:2])
     need("v", k_uo)
-    for q in range(2):
-        k_uf = done("vs", V.tensor_scalar(T.uofs[:, 3 * q:3 * q + 3], T.uplo[:, 3 * q:3 * q + 3], OC * q, None, ADD))
-    done("vs", V.memset(T.lf[:, 4 * UN:4 * UN + 4], 0.0))
-    k_z0 = done("vs", V.memset(T.rf[:, 4 * UN:4 * UN + 4], 0.0))
+    k_uf = copy("v", T.uofs[:, 0:3], T.uplo[:])
+    need("v", k_d0, k_bf)
+    k_mk = scalar(T.mask[:], T.d0[:], T.bitf[:, 0:1], None, AluOpType.is_equal)
     need("v", k_uf, k_win, k_wv)
-    k_sc = done("vs", V.tensor_copy(T.win[:].indirect(T.uofs[:]), T.wv[:]))
+    k_sc = copy("v", T.win[:].indirect(T.uofs[:, 0:3]), T.wv[:])
 
-    far, near = UN * (1 - half), UN * half
-    for t in (0, 2):
-        need("v", k_acc[t])
-        k_mv = done("vs", V.tensor_copy(T.mt[:, t:4 * UN:4], T.px[:, 512 * t + far:512 * t + far + UN]))
-    for t in (1, 3):
-        need("s", k_acc[t])
-        k_ms = done("ss", S.activation(T.mt[:, t:4 * UN:4], T.px[:, 512 * t + far:512 * t + far + UN], COPY))
-    need("v", k_mv, k_ms, k_mt)
-    k_qm = done("vs", V.quantize_mx(T.qm[:], T.sm[:], T.mt[:]))
+    def near_spread(k, x, n, *toks):
+        need("v", k_po, k_zn[k], *toks)
+        return copy("v", T.nt[:, 4 * WD * k:4 * WD * (k + 1)].indirect(T.pofs[:, 4 * x:4 * (x + n)]), T.zn[:, 64 * x:64 * (x + n)])
+
+    def near_tile(k, tok):
+        need("v", tok)
+        return quantise(T.qn[:, WD * k:WD * (k + 1)], T.sn[:, WD * k:WD * (k + 1)], T.nt[:, 4 * WD * k:4 * WD * (k + 1)])
+
+    def decode(t, out, c, start, stop, n=MINC):
+        e = EAT + 128 * t
+        return done("ts", P.matmul_mx(out[:, 512 * t:512 * t + n], T.land[:, e:e + 128], T.lsc[:, e:e + 128], T.land[:, c:c + n], T.lsc[:, c:c + n], start, stop))
+
+    def far_sum(j, stop):
+        return [decode(t, T.px, tile_at(j) + (0 if low else CAP), False, stop) for t in range(4)]
+
+    def near_codes(j, n):
+        return [decode(t, T.py, tile_at(j) + (UN if low else 0), True, True, n) for t in range(4)]
+
+    def pair_near(qs, s, toks):
+        return [tok for t in range(4) for e in range(2) for tok in near_cast("." * t + qs[t], behind[s] + e, T.py, TILE * e, toks)]
+
+    n8 = len(topo.engines(peers[mate], core))
+    nh = len(topo.engines(helper, core))
+    need("t", k_qbo, k_c0, *k_own)
+    for i in range(4):
+        product(T.px, i, T.qbo, T.sbo, True, False)
+    need("t", *k_second, ("earr", 2 * nh), ("arr4", 2 * n8))
+    k_mate = near_cast("ssss", mate, T.py, 0, near_codes(4, MINC))
+    k_qn = [near_tile(0, near_spread(0, lows[pair], 2, *(k_own + k_mate)))]
+    far_sum(4, False)
+    need("t", ("arr2", n8), ("arr3", n8), *k_mate)
+    k_ca = pair_near("ssss", 0, near_codes(2, MINC))
+    k_sp = near_spread(1, behind[0], 2, *k_ca)
+    far_sum(2, False)
+    need("t", ("arr0", n8), ("arr1", n8))
+    k_acc = far_sum(0, True)
+    need("t", *k_ca)
+    k_near = near_codes(0, MINC)
+
+    def fold(q, t):
+        need(q, k_acc[t])
+        return copy(q, T.fold[:, UN * t:UN * t + UN], T.px[:, 512 * t + TILE:512 * t + TILE + UN])
+
+    for t in range(4):
+        need("v", fold("s", t))
+        k_mv = done("vs", V.tensor_tensor(T.h[:, t:4 * UN:4], T.px[:, 512 * t:512 * t + UN], T.fold[:, UN * t:UN * t + UN], ADD))
+    need("v", k_mv)
+    k_qm = quantise(T.qm[:], T.sm[:], T.h[:, 0:512])
     other = T.cores[(rank + H) % (2 * H)]
     need("g", k_qm)
-    sent += write(other, T.sem.xarr, 0, UN, T.qm, T.sm, 0)
+    sent += write(other, T.sem.xarr, 0, UN, T.qm, T.sm)
 
-    need("v", k_d0, k_bf)
-    k_mk = done("vs", V.tensor_scalar(T.mask[:], T.d0[:], T.bitf[:, 2:3], None, AluOpType.is_equal))
+    k_qn.append(near_tile(1, k_sp))
+    k_cb = pair_near("sssv", 1, k_near)
+    k_qn.append(near_tile(2, near_spread(2, behind[1], 2, *k_cb)))
     need("v", k_mk, k_sc)
-    k_dm = done("vs", V.tensor_tensor(T.dm[:], T.win[:, 0:2 * OC], T.mask[:], MULT))
+    k_dm = done("vs", V.tensor_tensor(T.dm[:], T.win[:, 0:OC], T.mask[:], MULT))
     need("v", k_dm)
     k_ds = done("vs", V.tensor_tensor_scan(T.ds[:], T.d0[:], T.dm[:], 0.0, AluOpType.min, ADD))
     need("v", k_ds)
-    k_io = {}
-    for q in (host, 1 - host):
-        k_io[q] = done("vs", V.tensor_scalar(T.iofs[:, 22 * q:22 * q + 21], T.ds[:, OC * q + 3:OC * q + OC:4], 4, T.bitf[:, 3:4], MULT, ADD))
+    k_io = scalar(T.iofs[:, 0:21], T.ds[:, 3:OC:4], 4, T.bitf[:, 1:2], MULT, ADD)
+    need("t", ("warr", 2 * nh), *k_cb)
+    for k in range(3):
+        need("t", k_qn[k])
+        k_sum = [done("ts", P.matmul_mx(T.py[:, 512 * u:512 * u + WD], T.qw[:, 128 * u:128 * u + 128], T.sw[:, 128 * u:128 * u + 128],
+                                        T.qn[:, WD * k:WD * (k + 1)], T.sn[:, WD * k:WD * (k + 1)], k == 0, k == 2)) for u in range(2)]
+    k_y = []
+    for u, q in enumerate("sv"):
+        need(q, k_sum[u])
+        k_y.append(copy(q, T.yacc[:, u:4 * OC:2], T.py[:, 512 * u:512 * u + WD]))
 
-    for t in (1, 3, 0, 2):
-        if t == 0:
-            need("s", k_mv)
-        k_lf = done("ss", S.activation(T.lf[:, t:4 * UN:4], T.px[:, 512 * t + near:512 * t + near + UN], COPY))
-    need("s", k_lf, k_z0, k_io[host])
-    k_ya = done("ss", S.activation(T.yacc[:], T.lf[:].indirect(T.iofs[:, 22 * host:22 * host + 21]), COPY))
-
-    need("t", k_zc[5], ("xarr", arrivals(other)))
-    k_r = [decode(t, T.py, T.land, T.lsc, 0, True, True) for t in range(4)]
-    for t in (0, 2):
-        need("v", k_r[t])
-        k_rv = done("vs", V.tensor_copy(T.rf[:, t:4 * UN:4], T.py[:, 512 * t:512 * t + UN]))
-    for t in (1, 3):
-        need("s", k_r[t])
-        k_rs = done("ss", S.activation(T.rf[:, t:4 * UN:4], T.py[:, 512 * t:512 * t + UN], COPY))
-    need("v", k_rv, k_rs, k_ya, k_z0, k_io[1 - host])
-    q = 22 * (1 - host)
+    need("t", ("xarr", 2 * len(topo.engines(other, core))), k_mv)
+    k_r = [decode(t, T.px, 0, True, True) for t in range(4)]
+    for t, q in enumerate("svvv"):
+        need(q, k_r[t])
+        k_y.append(copy(q, T.rf[:, t:4 * UN:4], T.px[:, 512 * t:512 * t + UN]))
+    need("v", k_z0, k_io, *k_y)
     for lo, hi, queue in ((0, CUT, "y"), (CUT, 21, "s")):
-        tok = done("vs", V.tensor_tensor(T.yo[:, 16 * lo:16 * hi], T.rf[:].indirect(T.iofs[:, q + lo:q + hi]), T.yacc[:, 16 * lo:16 * hi], ADD))
-        need(queue, tok)
+        need(queue, done("vs", V.tensor_tensor(T.yo[:, 16 * lo:16 * hi], T.rf[:].indirect(T.iofs[:, lo:hi]), T.yacc[:, 16 * lo:16 * hi], ADD)))
         queues[queue].dma_start(T.y[:, 16 * lo:16 * hi], T.yo[:, 16 * lo:16 * hi]).then_inc(T.sem.stored, 16)
 
     need("g", ("sent", sent), ("vs", count["vs"]), ("ss", count["ss"]), ("ts", count["ts"]), ("gs", count["gs"]), ("stored", 32))

import numpy as np
from concourse.bass import DstId, RemoteDMATransfer
from concourse.mybir import dt, AluOpType, ActivationFunctionType

UN, OC, H, CAP = 48, 84, 6, 16
TILE = UN + CAP
MINC = 128
ZAT = UN + 5 * TILE
EAT = ZAT + TILE
ABIG = 1536
CUT = 10
H0, H2, H1 = 192, 448, 960
WD = 2 * OC

F32, BF, I32, U16, X4, U8 = "float32", "bfloat16", "int32", "uint16", "float8_e4m3fn_x4", "uint8"
SCRATCH = {
    "lists": ("sbuf", [128, 24], I32), "late": ("sbuf", [128, 12], I32),
    "ofs": ("sbuf", [128, 96], U16), "g2": ("sbuf", [128, 10], U16), "e01": ("sbuf", [128, 6], I32),
    "e80": ("sbuf", [128, 6], I32), "ue": ("sbuf", [128, 6], I32), "sofs": ("sbuf", [128, 16], U16),
    "p8": ("sbuf", [128, 6], I32), "pe": ("sbuf", [128, 6], I32), "pofs": ("sbuf", [128, 24], U16),
    "bt": ("sbuf", [128, 768], BF), "at": ("sbuf", [128, 2048], BF),
    "bc1": ("sbuf", [128, 128], BF), "bp": ("sbuf", [128, 512], BF), "bc2": ("sbuf", [128, 512], BF), "bo": ("sbuf", [128, 512], BF),
    "qa": ("sbuf", [128, 512], X4), "sa": ("sbuf", [128, 512], U8),
    "qb1": ("sbuf", [128, 128], X4), "sb1": ("sbuf", [128, 128], U8),
    "qb2": ("sbuf", [128, 128], X4), "sb2": ("sbuf", [128, 128], U8),
    "qbo": ("sbuf", [128, 128], X4), "sbo": ("sbuf", [128, 128], U8),
    "ones": ("sbuf", [128, 520], BF), "strip": ("sbuf", [128, 520], BF), "zt": ("sbuf", [128, 512], BF),
    "wt": ("sbuf", [128, 2 * 512], BF),
    "qe": ("sbuf", [128, TILE + 512], X4), "se": ("sbuf", [128, TILE + 512], U8),
    "qw": ("sbuf", [128, 256], X4), "sw": ("sbuf", [128, 256], U8),
    "zc": ("sbuf", [128, 256], BF), "h": ("sbuf", [128, H1 + 512], BF),
    "qh": ("sbuf", [128, 3 * MINC], X4), "sh": ("sbuf", [128, 3 * MINC], U8),
    "land": ("sbuf", [128, EAT + 512], X4), "lsc": ("sbuf", [128, EAT + 512], U8),
    "fold": ("sbuf", [128, 4 * UN], F32), "qm": ("sbuf", [128, 128], X4), "sm": ("sbuf", [128, 128], U8),
    "zn": ("sbuf", [128, H * 64], BF), "nt": ("sbuf", [128, 12 * WD], BF),
    "qn": ("sbuf", [128, 3 * WD], X4), "sn": ("sbuf", [128, 3 * WD], U8),
    "rf": ("sbuf", [128, 4 * UN + 4], F32), "yacc": ("sbuf", [128, 4 * OC], F32), "yo": ("sbuf", [128, 4 * OC], F32),
    "pc": ("sbuf", [128, 1], I32), "bits": ("sbuf", [128, 4], I32), "bitf": ("sbuf", [128, 4], F32),
    "dump": ("sbuf", [128, 3], I32), "neg": ("sbuf", [128, 3], I32), "uplo": ("sbuf", [128, 3], I32),
    "uofs": ("sbuf", [128, 4], U16), "wv": ("sbuf", [128, UN], F32), "win": ("sbuf", [128, 260], F32),
    "d0": ("sbuf", [128, OC], F32), "mask": ("sbuf", [128, OC], F32), "dm": ("sbuf", [128, OC], F32),
    "ds": ("sbuf", [128, OC], F32), "iofs": ("sbuf", [128, 22], U16),
    "px": ("psum", [128, 2048], F32), "py": ("psum", [128, 2048], F32),
}
SEMAPHORES = ["gs", "vs", "ss", "ts", "ldl", "ldlate", "ldb", "lda0", "lda1", "stored", "sent", "xarr", "earr", "warr"] + ["arr%d" % k for k in range(5)]


def helper_of(c, T, topo):
    return min(o for o in topo.cores_of(c) if o not in T.cores and topo.die(o) == topo.die(c))


def bits_of(engines):
    return sum(1 << e for e in engines)


def tile_at(j):
    return UN + TILE * j


def helper_program(g, core, target, T, topo):
    V = g.vector
    rid, pid = topo.addr(target, core)
    eng = topo.engines(core, target)
    V.memset(T.ones[:], 1.0).then_inc(T.sem.vs, 1)
    V.memset(T.zt[:], 0.0).then_inc(T.sem.vs, 1)
    g.wait_ge(T.sem.vs, 1)
    g.affine_select(T.strip[:], T.ones[:], [[1, 520]], AluOpType.is_equal, 0.0, -4, -4).then_inc(T.sem.gs, 1)
    V.wait_ge(T.sem.vs, 2)
    V.quantize_mx(T.qe[:, 0:MINC], T.se[:, 0:MINC], T.zt[:]).then_inc(T.sem.vs, 1)
    V.wait_ge(T.sem.gs, 1)
    V.wait_ge(T.sem.vs, 3)
    for t in range(4):
        c = TILE + 128 * t
        V.quantize_mx(T.qe[:, c:c + 128], T.se[:, c:c + 128], T.strip[:, 4 - t:516 - t]).then_inc(T.sem.vs, 1)
    g.wait_ge(T.sem.vs, 7)
    g.remote_dma(T.land[:, ZAT:EAT + 512].bitcast(dt.uint8), T.qe[:].bitcast(dt.uint8), T.sem.earr, T.sem.sent, pid, rid, bits_of(eng))
    g.remote_dma(T.lsc[:, ZAT:EAT + 512], T.se[:], T.sem.earr, T.sem.sent, pid, rid, bits_of(eng))
    for u in range(2):
        V.tensor_tensor(T.wt[:, 512 * u:512 * u + 512], T.strip[:, 4 - 2 * u:516 - 2 * u], T.strip[:, 3 - 2 * u:515 - 2 * u], AluOpType.add).then_inc(T.sem.vs, 1)
    V.wait_ge(T.sem.vs, 9)
    V.quantize_mx(T.qw[:], T.sw[:], T.wt[:]).then_inc(T.sem.vs, 1)
    g.wait_ge(T.sem.vs, 10)
    g.remote_dma(T.qw[:].bitcast(dt.uint8), T.qw[:].bitcast(dt.uint8), T.sem.warr, T.sem.sent, pid, rid, bits_of(eng))
    g.remote_dma(T.sw[:], T.sw[:], T.sem.warr, T.sem.sent, pid, rid, bits_of(eng))
    g.wait_ge(T.sem.sent, 4 * len(eng))
    g.wait_ge(T.sem.gs, 1)


def rank_program(g, core, T, topo):
    rank = T.rank_of(core)
    if rank is None:
        for c in T.cores:
            if helper_of(c, T, topo) == core:
                helper_program(g, core, c, T, topo)
        return
    V, S, P, Y = g.vector, g.scalar, g.tensor, g.sync
    COPY = ActivationFunctionType.Copy
    ADD, MULT, AND, SHR = AluOpType.add, AluOpType.mult, AluOpType.bitwise_and, AluOpType.logical_shift_right
    FLT = {"allow_small_or_imprecise_dtypes": True}
    half, me = rank // H, rank % H
    peers = [T.cores[half * H + x] for x in range(H)]
    host = topo.host(core)
    helper = helper_of(core, T, topo)
    mate = [x for x in range(H) if topo.mates(core, peers[x])][0]
    lows = [x for x in range(H) if x + 1 < H and topo.mates(peers[x], peers[x + 1])]
    pair = lows.index(min(me, mate))
    ahead = [lows[(pair + s) % 3] for s in (1, 2)]
    behind = [lows[(pair - s) % 3] for s in (1, 2)]
    NEAR, FAR = H * half, H * (1 - half)
    low = me < mate

    count = {"gs": 0, "vs": 0, "ss": 0, "ts": 0}
    queues = {"g": g, "v": V, "s": S, "t": P, "y": Y}
    known = {q: {} for q in queues}

    def done(sem, ins):
        ins.then_inc(T.sem[sem], 1)
        count[sem] += 1
        return (sem, count[sem])

    def need(q, *tokens):
        best = {}
        for sem, n in tokens:
            best[sem] = max(n, best.get(sem, 0))
        for sem, n in best.items():
            if known[q].get(sem, 0) < n:
                queues[q].wait_ge(T.sem[sem], n)
                known[q][sem] = n

    def copy(q, out, in_):
        return done("vs", V.tensor_copy(out, in_)) if q == "v" else done("ss", S.activation(out, in_, COPY))

    def scalar(out, in_, *rest):
        return done("vs", V.tensor_scalar(out, in_, *rest))

    def quantise(codes, scales, tile):
        return done("vs", V.quantize_mx(codes, scales, tile))

    def zero(out, n):
        return done("ss", S.activation(out, T.bt[:, 0:n], COPY, scale=0.0))

    for k in range(2):
        Y.dma_start(T.lists[16 * k:16 * k + 16, 0:12], T.send[:]).then_inc(T.sem.ldl, 16)
        S.dma_start(T.lists[16 * k:16 * k + 16, 12:24], T.un[:]).then_inc(T.sem.ldl, 16)
    Y.dma_start(T.bt[:], T.b[:]).then_inc(T.sem.ldb, 16)
    Y.dma_start(T.at[:, 0:ABIG], T.a[:, 0:ABIG]).then_inc(T.sem.lda0, 16)
    Y.dma_start(T.at[:, ABIG:2048], T.a[:, ABIG:2048]).then_inc(T.sem.lda1, 16)
    for k in range(2):
        Y.dma_start(T.late[16 * k:16 * k + 16, 0:H], T.place[:, NEAR:NEAR + H]).then_inc(T.sem.ldlate, 16)
        Y.dma_start(T.late[16 * k:16 * k + 16, H:2 * H], T.upl[:]).then_inc(T.sem.ldlate, 16)
    LL, LATE, LB, LA0, LA1 = ("ldl", 64), ("ldlate", 64), ("ldb", 16), ("lda0", 16), ("lda1", 16)

    k_zh2 = done("gs", g.iota(T.h[:, H2:H2 + 512], [[0, 512]], 0, 0, **FLT))
    k_e80 = done("gs", g.iota(T.e80[:], [[0, 3], [TILE + CAP, 2]], 0, 0))
    k_pc = done("gs", g.iota(T.pc[:], [[0, 1]], 0, 1))
    k_e01 = done("gs", g.iota(T.e01[:], [[0, 3], [1, 2]], 0, 0))
    k_dump = done("gs", g.iota(T.dump[:], [[-16, 3]], -OC, -1))
    k_wv = done("gs", g.iota(T.wv[:], [[1, UN]], 0, 0, **FLT))
    k_d0 = done("gs", g.iota(T.d0[:], [[0, OC // 4], [1000, 4]], 0, 0, **FLT))
    k_bp0 = done("vs", V.memset(T.bp[:], 0.0))
    k_zbo = done("vs", V.memset(T.bo[:], 0.0))
    k_z0 = done("vs", V.memset(T.rf[:, 4 * UN:4 * UN + 4], 0.0))
    k_win = done("vs", V.memset(T.win[:, 0:OC], float(UN)))
    need("s", k_bp0)
    k_zh1 = copy("s", T.h[:, H1:H1 + 512], T.bp[:])

    need("v", LL)
    for p0 in (32, 64, 96):
        k_l = copy("v", T.lists[p0:p0 + 32, :], T.lists[0:32, :])
    need("v", k_l)
    for s, x in enumerate(ahead):
        for i, c in enumerate((FAR, NEAR)):
            k_g2 = scalar(T.g2[:, 4 * s + 2 * i:4 * s + 2 * i + 2], T.lists[:, c + x:c + x + 2], 4, None, MULT)
    for t in range(4):
        k_ofs = scalar(T.ofs[:, t:96:4], T.lists[:], 4, t, MULT, ADD)
    c = NEAR + lows[pair]
    k_g1 = scalar(T.g2[:, 8:10], T.lists[:, c:c + 2], 4, None, MULT)

    def picks(c):
        return T.ofs[:, 4 * c:4 * c + 4]

    def places(c):
        return T.ofs[:, 48 + 4 * c:52 + 4 * c]

    f0, n0, t0, o0 = (2 * CAP, 0, CAP, 0) if low else (0, UN, 0, TILE)
    need("s", LB, k_zh1, k_g1)
    for t in range(4):
        k_bn = copy("s", T.bp[:, 4 * n0 + t:4 * n0 + 128:4], T.bt[:, t:768].indirect(T.g2[:, 8:10]))
    need("s", k_g2)
    for t in range(4):
        k_bc2 = copy("s", T.bc2[:, t:512:4], T.bt[:, t:768].indirect(T.g2[:, 0:8]))
    need("v", LB, k_ofs)
    k_bc1 = copy("v", T.bc1[:, 0:64], T.bt[:].indirect(picks(FAR + mate)))
    need("v", k_e80)
    k_ue = done("vs", V.tensor_tensor(T.ue[:], T.lists[:, 12 + FAR:12 + FAR + H], T.e80[:], ADD))
    need("v", k_bc1, k_bp0, k_zh1)
    k_bp = copy("v", T.bp[:, 4 * f0:4 * (f0 + UN)].indirect(places(FAR + mate)), T.bc1[:, 0:64])

    def pair_places(s):
        for t in range(4):
            tok = scalar(T.sofs[:, 8 * s + 2 * t:8 * s + 2 * t + 2], T.ue[:, ahead[s]:ahead[s] + 2], 4, t, MULT, ADD)
        return tok

    need("v", k_ue)
    k_so = [pair_places(0)]
    need("v", LA0)
    k_qa0 = quantise(T.qa[:, 0:ABIG // 4], T.sa[:, 0:ABIG // 4], T.at[:, 0:ABIG])
    need("v", k_bp, k_bn)
    k_qb1 = quantise(T.qb1[:], T.sb1[:], T.bp[:])
    need("v", LA1)
    k_qa1 = quantise(T.qa[:, ABIG // 4:512], T.sa[:, ABIG // 4:512], T.at[:, ABIG:2048])
    need("v", k_bc2)
    k_qb2 = quantise(T.qb2[:], T.sb2[:], T.bc2[:])

    def product(out, i, codes, scales, start, stop):
        return done("ts", P.matmul_mx(out[:, 512 * i:512 * i + MINC], T.qa[:, 128 * i:128 * i + 128], T.sa[:, 128 * i:128 * i + 128],
                                      codes[:], scales[:], start, stop))

    for i in range(4):
        need("t", k_qb1, k_qa1 if i == 3 else k_qa0)
        need("v", product(T.px, i, T.qb1, T.sb1, True, True))
        k_c0 = copy("v", T.h[:, H0 + i:H0 + 4 * TILE:4], T.px[:, 512 * i + t0:512 * i + t0 + TILE])
    need("t", k_qb2)
    k_py = [product(T.py, i, T.qb2, T.sb2, True, True) for i in range(4)]
    need("v", k_c0, k_zh2)
    k_h = [quantise(T.qh[:, 0:MINC], T.sh[:, 0:MINC], T.h[:, H0:H0 + 512])]

    def near_cast(qs, x, bank, c, toks):
        out = {}
        for t, q in enumerate(qs):
            if q != ".":
                need(q, toks[t])
                out[q] = copy(q, T.zn[:, 64 * x + 16 * t:64 * x + 16 * t + 16], bank[:, 512 * t + c:512 * t + c + CAP])
        return list(out.values())

    def pair_cast(q, s, t, tok):
        c, at = 512 * t + 64 * s, (H1, H2)[s] + 4 * UN
        need(q, tok, k_zh1, k_zh2, *k_h[:s])
        copy(q, T.zc[:, 128 * s + 32 * t:128 * s + 32 * t + 32], T.py[:, c:c + 32])
        return copy(q, T.h[:, at + t:at + 128:4], T.py[:, c + 32:c + 64])

    k_first = [pair_cast("s", 0, t, k_py[t]) for t in range(4)]
    k_second = [pair_cast("s", 1, t, k_py[t]) for t in range(4)]
    for s, (at, toks) in enumerate(((H1, k_first), (H2, k_second))):
        if s == 0:
            k_so.append(pair_places(1))
        need("v", k_so[s], *toks)
        need("v", copy("v", T.h[:, at:at + 512].indirect(T.sofs[:, 8 * s:8 * s + 8]), T.zc[:, 128 * s:128 * s + 128]))
        k_h.append(quantise(T.qh[:, MINC * (s + 1):MINC * (s + 2)], T.sh[:, MINC * (s + 1):MINC * (s + 2)], T.h[:, at:at + 512]))

    def write(to, sem, at, n, codes, scales):
        rid, pid = topo.addr(to, core)
        eng = topo.engines(core, to)
        g.remote_dma(T.land[:, at:at + n].bitcast(dt.uint8), codes[:, 0:n].bitcast(dt.uint8), sem, T.sem.sent, pid, rid, bits_of(eng))
        g.remote_dma(T.lsc[:, at:at + n], scales[:, 0:n], sem, T.sem.sent, pid, rid, bits_of(eng))
        return 2 * len(eng)

    need("g", k_h[0])
    sent = write(peers[mate], T.sem.arr4, tile_at(4), TILE, T.qh, T.sh)
    for s, x in enumerate(ahead):
        need("g", k_h[s + 1])
        j = 2 * (1 - s) + (0 if low else 1)
        for plane in range(2):
            ts = []
            for e in range(2):
                rid, pid = topo.addr(peers[x + e], core)
                eng = topo.engines(core, peers[x + e])
                n, lo = len(eng) // 2, MINC * (s + 1) + TILE * e
                if plane:
                    src, dst = T.sh[:, lo:lo + TILE], T.lsc[:, tile_at(j):tile_at(j) + TILE]
                else:
                    src, dst = T.qh[:, lo:lo + TILE].bitcast(dt.uint8), T.land[:, tile_at(j):tile_at(j) + TILE].bitcast(dt.uint8)
                ts.append(RemoteDMATransfer(dst_ids=[DstId(rid=rid, pnc=pid)], dma_engine_mask=bits_of(eng[n * e:n * e + n]),
                                            remote_sem=T.sem["arr%d" % j], srcs=[src], dsts=[dst]))
                sent += n
            g.remote_dma_fused(ts, local_sem=T.sem.sent)

    k_bco = copy("s", T.bc1[:, 64:128], T.bt[:].indirect(picks(FAR + me)))
    k_own = near_cast("ssss", me, T.px, o0, [k_c0] * 4)
    k_zn = [zero(T.nt[:, 4 * WD * k:4 * WD * (k + 1)], 4 * WD) for k in range(2)]
    k_zn.append(done("gs", g.iota(T.nt[:, 8 * WD:12 * WD], [[0, 4 * WD]], 0, 0, **FLT)))
    need("v", k_bco, k_zbo)
    k_bo = copy("v", T.bo[:, 0:4 * UN].indirect(places(FAR + me)), T.bc1[:, 64:128])
    need("v", LATE)
    for p0 in (32, 64, 96):
        k_l = copy("v", T.late[p0:p0 + 32, :], T.late[0:32, :])
    need("v", k_bo)
    k_qbo = quantise(T.qbo[:], T.sbo[:], T.bo[:])

    q = H + 3 * (1 - host)
    need("v", k_l, k_dump)
    k_p8 = scalar(T.p8[:], T.late[:, 0:H], 8, None, MULT)
    k_ng = done("vs", V.tensor_tensor(T.neg[:], T.late[:, q:q + 3], T.dump[:], MULT))
    need("v", k_p8, k_e01)
    k_pe = done("vs", V.tensor_tensor(T.pe[:], T.p8[:], T.e01[:], ADD))
    need("v", k_ng)
    k_uo = done("vs", V.tensor_tensor(T.uplo[:], T.neg[:], T.late[:, q:q + 3], AluOpType.max))
    need("v", k_pc)
    for c, (shift, mask) in enumerate(((2, 3), (0, 3))):
        k_b = scalar(T.bits[:, c:c + 1], T.pc[:], shift, mask, SHR, AND)
    need("v", k_pe)
    for t in range(4):
        k_po = scalar(T.pofs[:, t:24:4], T.pe[:], 2 * t, None, ADD)
    need("v", k_b)
    scalar(T.bitf[:, 0:1], T.bits[:, 0:1], 1000, None, MULT)
    k_bf = copy("v", T.bitf[:, 1:2], T.bits[:, 1:2])
    need("v", k_uo)
    k_uf = copy("v", T.uofs[:, 0:3], T.uplo[:])
    need("v", k_d0, k_bf)
    k_mk = scalar(T.mask[:], T.d0[:], T.bitf[:, 0:1], None, AluOpType.is_equal)
    need("v", k_uf, k_win, k_wv)
    k_sc = copy("v", T.win[:].indirect(T.uofs[:, 0:3]), T.wv[:])

    def near_spread(k, x, n, *toks):
        need("v", k_po, k_zn[k], *toks)
        return copy("v", T.nt[:, 4 * WD * k:4 * WD * (k + 1)].indirect(T.pofs[:, 4 * x:4 * (x + n)]), T.zn[:, 64 * x:64 * (x + n)])

    def near_tile(k, tok):
        need("v", tok)
        return quantise(T.qn[:, WD * k:WD * (k + 1)], T.sn[:, WD * k:WD * (k + 1)], T.nt[:, 4 * WD * k:4 * WD * (k + 1)])

    def decode(t, out, c, start, stop, n=MINC):
        e = EAT + 128 * t
        return done("ts", P.matmul_mx(out[:, 512 * t:512 * t + n], T.land[:, e:e + 128], T.lsc[:, e:e + 128], T.land[:, c:c + n], T.lsc[:, c:c + n], start, stop))

    def far_sum(j, stop):
        return [decode(t, T.px, tile_at(j) + (0 if low else CAP), False, stop) for t in range(4)]

    def near_codes(j, n):
        return [decode(t, T.py, tile_at(j) + (UN if low else 0), True, True, n) for t in range(4)]

    def pair_near(qs, s, toks):
        return [tok for t in range(4) for e in range(2) for tok in near_cast("." * t + qs[t], behind[s] + e, T.py, TILE * e, toks)]

    n8 = len(topo.engines(peers[mate], core))
    nh = len(topo.engines(helper, core))
    need("t", k_qbo, k_c0, *k_own)
    for i in range(4):
        product(T.px, i, T.qbo, T.sbo, True, False)
    need("t", *k_second, ("earr", 2 * nh), ("arr4", 2 * n8))
    k_mate = near_cast("ssss", mate, T.py, 0, near_codes(4, MINC))
    k_qn = [near_tile(0, near_spread(0, lows[pair], 2, *(k_own + k_mate)))]
    far_sum(4, False)
    need("t", ("arr2", n8), ("arr3", n8), *k_mate)
    k_ca = pair_near("ssss", 0, near_codes(2, MINC))
    k_sp = near_spread(1, behind[0], 2, *k_ca)
    far_sum(2, False)
    need("t", ("arr0", n8), ("arr1", n8))
    k_acc = far_sum(0, True)
    need("t", *k_ca)
    k_near = near_codes(0, MINC)

    def fold(q, t):
        need(q, k_acc[t])
        return copy(q, T.fold[:, UN * t:UN * t + UN], T.px[:, 512 * t + TILE:512 * t + TILE + UN])

    for t in range(4):
        need("v", fold("s", t))
        k_mv = done("vs", V.tensor_tensor(T.h[:, t:4 * UN:4], T.px[:, 512 * t:512 * t + UN], T.fold[:, UN * t:UN * t + UN], ADD))
    need("v", k_mv)
    k_qm = quantise(T.qm[:], T.sm[:], T.h[:, 0:512])
    other = T.cores[(rank + H) % (2 * H)]
    need("g", k_qm)
    sent += write(other, T.sem.xarr, 0, UN, T.qm, T.sm)

    k_qn.append(near_tile(1, k_sp))
    k_cb = pair_near("sssv", 1, k_near)
    k_qn.append(near_tile(2, near_spread(2, behind[1], 2, *k_cb)))
    need("v", k_mk, k_sc)
    k_dm = done("vs", V.tensor_tensor(T.dm[:], T.win[:, 0:OC], T.mask[:], MULT))
    need("v", k_dm)
    k_ds = done("vs", V.tensor_tensor_scan(T.ds[:], T.d0[:], T.dm[:], 0.0, AluOpType.min, ADD))
    need("v", k_ds)
    k_io = scalar(T.iofs[:, 0:21], T.ds[:, 3:OC:4], 4, T.bitf[:, 1:2], MULT, ADD)
    need("t", ("warr", 2 * nh), *k_cb)
    for k in range(3):
        need("t", k_qn[k])
        k_sum = [done("ts", P.matmul_mx(T.py[:, 512 * u:512 * u + WD], T.qw[:, 128 * u:128 * u + 128], T.sw[:, 128 * u:128 * u + 128],
                                        T.qn[:, WD * k:WD * (k + 1)], T.sn[:, WD * k:WD * (k + 1)], k == 0, k == 2)) for u in range(2)]
    k_y = []
    for u, q in enumerate("sv"):
        need(q, k_sum[u])
        k_y.append(copy(q, T.yacc[:, u:4 * OC:2], T.py[:, 512 * u:512 * u + WD]))

    need("t", ("xarr", 2 * len(topo.engines(other, core))), k_mv)
    k_r = [decode(t, T.px, 0, True, True) for t in range(4)]
    for t, q in enumerate("svvv"):
        need(q, k_r[t])
        k_y.append(copy(q, T.rf[:, t:4 * UN:4], T.px[:, 512 * t:512 * t + UN]))
    need("v", k_z0, k_io, *k_y)
    for lo, hi, queue in ((0, CUT, "y"), (CUT, 21, "s")):
        need(queue, done("vs", V.tensor_tensor(T.yo[:, 16 * lo:16 * hi], T.rf[:].indirect(T.iofs[:, lo:hi]), T.yacc[:, 16 * lo:16 * hi], ADD)))
        queues[queue].dma_start(T.y[:, 16 * lo:16 * hi], T.yo[:, 16 * lo:16 * hi]).then_inc(T.sem.stored, 16)

    need("g", ("sent", sent), ("vs", count["vs"]), ("ss", count["ss"]), ("ts", count["ts"]), ("gs", count["gs"]), ("stored", 32))
